import numpy as np
import ml_dtypes


def mxq(x, axis, fmt="e4m3"):
    dtype, down = {"e4m3": (ml_dtypes.float8_e4m3fn, 7), "e5m2": (ml_dtypes.float8_e5m2, 14)}[fmt]
    v = np.moveaxis(np.asarray(x, np.float32).astype(ml_dtypes.bfloat16).astype(np.float64), axis, -1)
    blocks = v.reshape(v.shape[:-1] + (-1, 32))
    amax = np.abs(blocks).max(-1, keepdims=True)
    byte = np.maximum(np.where(amax > 0, np.frexp(amax)[1] - 1 + 127, 0) - down, 1)
    scale = np.exp2(byte - 127.0)
    codes = (blocks / scale).astype(np.float32).astype(dtype).astype(np.float64)
    return np.moveaxis((codes * scale).reshape(v.shape), -1, axis)


WIDE = False


def mx_kscale(k):
    if not WIDE:
        return np.ones(k)
    levels = np.array([10, -10, 5, -5, 0])
    if k % 512:
        return np.exp2(np.random.permutation(np.resize(levels, k // 32))).repeat(32)
    a = np.empty((k // 512, 16))
    for p in range(k // 512):
        a[p, :8] = np.random.permutation(np.resize(levels, 8))
        for g in range(8):
            far = levels[np.abs(levels - a[p, g]) >= 10]
            a[p, g + 8] = far[np.random.randint(len(far))]
    return np.exp2(a.ravel()).repeat(32)


def f64(x):
    return np.asarray(x).astype(np.float64)


def striped8(idx):
    return np.concatenate([x.reshape(-1, 16).T for x in idx]).astype(np.uint16)


def runs(offs, k):
    lists = np.stack([offs[16 * r : 16 * r + 16].T.reshape(-1) for r in range(8)]).astype(np.int64)
    return lists[np.arange(k) % 512 // 64]


def pack_weight(w):
    k, n = w.shape
    w = f64(np.asarray(w, np.float32).astype(ml_dtypes.bfloat16)).reshape(k // 32, 32, n)
    amax = np.abs(w).max(1)
    byte = np.clip(np.where(amax > 0, np.frexp(amax)[1] - 1 + 127 - 7, 1), 1, 254)
    scaled = (w * np.exp2(127.0 - byte)[:, None, :]).reshape(k, n).astype(np.float32)
    words = np.ascontiguousarray(scaled.reshape(k // 512, 128, 4, n).transpose(0, 1, 3, 2)).astype(ml_dtypes.float8_e4m3fn).view(np.uint8)
    return words, np.ascontiguousarray(byte.astype(np.uint8).reshape(k // 512, 16, n))


def unpack_weight(words, scales):
    g, p, n, _ = words.shape
    vals = np.ascontiguousarray(words).view(ml_dtypes.float8_e4m3fn).astype(np.float64) * np.repeat(np.exp2(scales.astype(np.float64) - 127.0), 8, axis=1)[..., None]
    return vals.transpose(0, 1, 3, 2).reshape(g * 512, n)

def planes(y):
    n, m = y.shape
    v = y.astype(np.float32).astype(ml_dtypes.bfloat16).astype(np.float64).reshape(n // 32, 32, m)
    top = np.abs(v).max(1)
    byte = np.clip(np.where(top > 0, np.frexp(top)[1] - 1 + 127 - 7, 1), 1, 254)
    codes = (v * np.exp2(127.0 - byte)[:, None, :]).reshape(n, m).astype(np.float32).astype(ml_dtypes.float8_e4m3fn).view(np.uint8)
    words = codes.reshape(n // 512, 128, 4, m).transpose(0, 1, 3, 2)
    return np.ascontiguousarray(words), np.ascontiguousarray(byte.astype(np.uint8).reshape(n // 512, 16, m))


K, T, S, N, H = 512, 2048, 512, 512, 512


def setup_inputs():
    n = np.random.standard_normal
    s = mx_kscale(K)[:, None]
    u = mx_kscale(H)
    packed_xT = pack_weight(n((K, T)) * s)
    packed_w3 = pack_weight(n((H, N)) / np.sqrt(2 * H) / u[:, None])
    packed_w4 = pack_weight(n((H, N)) / np.sqrt(2 * H) / u[:, None])
    return {
        "x_words": packed_xT[0],
        "x_scales": packed_xT[1],
        "w1": (n((K, H)) / np.sqrt(K) / s * u).astype(np.float32),
        "w2": (n((K, H)) / np.sqrt(K) / s * u).astype(np.float32),
        "hr": (n((H, S)) * u[:, None]).astype(np.float32),
        "hi": (n((H, S)) * u[:, None]).astype(np.float32),
        "lr": np.random.uniform(-0.7, 0.7, (H, 1)).astype(np.float32),
        "li": np.random.uniform(-0.7, 0.7, (H, 1)).astype(np.float32),
        "w3_words": packed_w3[0],
        "w3_scales": packed_w3[1],
        "w4_words": packed_w4[0],
        "w4_scales": packed_w4[1],
        "offs": striped8(np.stack([np.random.permutation(T)[:S] for _ in range(8)])),
        "par": striped8(np.random.randint(0, S, (8, S))),
    }


def reference(x_words, x_scales, w1, w2, hr, hi, lr, li, w3_words, w3_scales, w4_words, w4_scales, offs, par):
    pr = f64(hr)[np.arange(H)[:, None], runs(par, H)]
    pi = f64(hi)[np.arange(H)[:, None], runs(par, H)]
    xq = unpack_weight(x_words, x_scales)[np.arange(K)[:, None], runs(offs, K)]
    br = mxq(f64(w1), 0, "e4m3").T @ xq
    z = f64(lr) * pr - (f64(li) * pi) + br
    bi = mxq(f64(w2), 0, "e4m3").T @ xq
    z2 = f64(lr) * pi + f64(li) * pr + bi
    out_0 = unpack_weight(w3_words, w3_scales).T @ mxq(z, 0, "e4m3") + unpack_weight(w4_words, w4_scales).T @ mxq(z2, 0, "e4m3")
    return (out_0,) + planes(out_0)

@@ -1,0 +1,228 @@
+from contextlib import ExitStack
+
+import concourse.mybir as mybir
+
+K, T, S, N, H = 512, 2048, 512, 512, 512
+FLOPS = 4 * 2 * 512 * 512 * 512
+
+F32 = mybir.dt.float32
+BF16 = mybir.dt.bfloat16
+I32 = mybir.dt.int32
+U32 = mybir.dt.uint32
+U16 = mybir.dt.uint16
+U8 = mybir.dt.uint8
+FP8X4 = mybir.dt.float8_e4m3fn_x4
+ALU = mybir.AluOpType
+COPY = mybir.ActivationFunctionType.Copy
+
+P = 128
+PACK = 4
+CHUNK = 128
+HALF = 256
+
+
+def tile_picked_lru8_none_po_kernel(
+    tc, x_words, x_scales, w1, w2, hr, hi, lr, li, w3_words, w3_scales, w4_words, w4_scales, offs, par, out_0, out_1, out_2
+):
+    nc = tc.nc
+    with ExitStack() as ctx:
+        held = ctx.enter_context(tc.tile_pool(name="held", bufs=1))
+        ring = ctx.enter_context(tc.tile_pool(name="ring", bufs=4))
+        psum_b = ctx.enter_context(tc.psum_pool(name="psum_b", bufs=3))
+        psum_o = ctx.enter_context(tc.psum_pool(name="psum_o", bufs=2))
+
+        def as_words(packed):
+            return packed[0].rearrange("p n t -> p (n t)").bitcast(I32)
+
+        offs_t = held.tile([P, S // 16], U16, name="offs_t")
+        par_t = held.tile([P, S // 16], U16, name="par_t")
+        lr_t = held.tile([P, PACK], F32, name="lr_t")
+        li_t = held.tile([P, PACK], F32, name="li_t")
+        xw = held.tile([P, T], U32, name="xw")
+        xs = held.tile([P, T], U8, name="xs")
+        xw_g = held.tile([P, S], U32, name="xw_g", align_bytes=64)
+        xs_g = held.tile([P, S], U8, name="xs_g", align_bytes=64)
+        xs_p = held.tile([P, S], U8, name="xs_p", align_bytes=64)
+        hr_t = [held.tile([P, S], F32, name="hr%d" % t) for t in range(PACK)]
+        hi_t = [held.tile([P, S], F32, name="hi%d" % t) for t in range(PACK)]
+        w_raw = [held.tile([P, PACK, H], F32, name="w_raw%d" % a) for a in range(2)]
+        w_bf = [held.tile([P, H * PACK], BF16, name="w_bf%d" % a, align_bytes=64) for a in range(2)]
+        w_q = [held.tile([P, H], U32, name="w_q%d" % a, align_bytes=64) for a in range(2)]
+        w_s = [held.tile([P, H], U8, name="w_s%d" % a, align_bytes=64) for a in range(2)]
+        v_raw = held.tile([P, 2, N], I32, name="v_raw", tag="z0", align_bytes=64)
+        v_q = held.tile([P, PACK, 2, P], U32, name="v_q", align_bytes=64)
+        vs_raw = held.tile([P, N], U8, name="vs_raw", tag="z1", align_bytes=64)
+        v_s = held.tile([P, N], U8, name="v_s", align_bytes=64)
+        win = [[held.tile([P, 2 * S], F32, name="win%d_%d" % (a, t)) for t in range(PACK)] for a in range(2)]
+        got = [held.tile([P, PACK, S], F32, name="got%d" % a) for a in range(2)]
+        y_q = held.tile([P, S], U32, name="y_q", align_bytes=64)
+        y_s = held.tile([P, S], U8, name="y_s", align_bytes=64)
+
+        hr_rows = hr.rearrange("(p t) s -> p t s", t=PACK)
+        hi_rows = hi.rearrange("(p t) s -> p t s", t=PACK)
+
+        warm = held.tile([P, 1], F32, name="warm")
+        warm2 = held.tile([P, 1], F32, name="warm2")
+        nc.vector.memset(warm[:], 0.0)
+        nc.scalar.activation(warm2[:], warm[:], COPY)
+        nc.vector.memset(xs[:].bitcast(I32), 0)
+        nc.gpsimd.memset(xs_p[:].bitcast(I32), 0)
+        nc.gpsimd.memset(vs_raw[:].bitcast(I32), 0)
+
+        def load_h(t):
+            nc.sync.dma_start(hr_t[t][:], hr_rows[:, t, :])
+            nc.sync.dma_start(hi_t[t][:], hi_rows[:, t, :])
+
+        def load_w(a):
+            nc.sync.dma_start(w_raw[a][:], (w1, w2)[a].rearrange("(p j) c -> p j c", j=PACK))
+
+        nc.sync.dma_start(li_t[:], li.rearrange("(p t) o -> p (t o)", t=PACK))
+        load_h(0)
+        nc.sync.dma_start(xs[0:P:8, :].bitcast(I32), x_scales[0].bitcast(I32))
+        nc.sync.dma_start(offs_t[:], offs)
+        nc.sync.dma_start(lr_t[:], lr.rearrange("(p t) o -> p (t o)", t=PACK))
+        nc.sync.dma_start(par_t[:], par)
+        load_h(1)
+        nc.sync.dma_start(xw[:].bitcast(I32), as_words(x_words))
+        load_h(2)
+        load_h(3)
+        load_w(0)
+        load_w(1)
+        nc.sync.dma_start(v_raw[:, 0, :], as_words(w3_words))
+        nc.sync.dma_start(v_raw[:, 1, :], as_words(w4_words))
+        def rotate_v(t):
+            col = slice(t, t + 1)
+            nc.scalar.activation(win[0][t][:, S:], hi_t[t][:], COPY, scale=li_t[:, col])
+            nc.scalar.activation(win[1][t][:, S:], hr_t[t][:], COPY, scale=li_t[:, col])
+            nc.vector.scalar_tensor_tensor(win[0][t][:, :S], hr_t[t][:], lr_t[:, col], win[0][t][:, S:], ALU.mult, ALU.subtract)
+            nc.vector.scalar_tensor_tensor(win[1][t][:, :S], hi_t[t][:], lr_t[:, col], win[1][t][:, S:], ALU.mult, ALU.add)
+
+        def rotate_g(t):
+            col = slice(t, t + 1)
+            u = ring.tile([P, S], F32, name="u")
+            v = ring.tile([P, S], F32, name="v")
+            nc.scalar.activation(win[0][t][:, S:], hr_t[t][:], COPY, scale=lr_t[:, col])
+            nc.scalar.activation(u[:], hi_t[t][:], COPY, scale=li_t[:, col])
+            nc.gpsimd.tensor_tensor(win[0][t][:, :S], win[0][t][:, S:], u[:], ALU.subtract)
+            nc.scalar.activation(win[1][t][:, S:], hi_t[t][:], COPY, scale=lr_t[:, col])
+            nc.scalar.activation(v[:], hr_t[t][:], COPY, scale=li_t[:, col])
+            nc.gpsimd.tensor_tensor(win[1][t][:, :S], win[1][t][:, S:], v[:], ALU.add)
+
+        def gather_h(a, t, lo, hi_col):
+            nc.vector.tensor_copy(got[a][:, t, lo:hi_col], win[a][t][:].indirect(par_t[:, lo // 16 : hi_col // 16]))
+
+        def cast_w(a):
+            nc.scalar.copy(
+                w_bf[a][:].rearrange("p (t m j) -> p m j t", t=PACK, j=PACK),
+                w_raw[a][:].rearrange("p j (m t) -> p m j t", t=PACK),
+            )
+
+        def quant_w(a):
+            nc.vector.quantize_mx(out=w_q[a][:].bitcast(FP8X4), scales=w_s[a][:], in_=w_bf[a][:])
+
+        nc.vector.tensor_copy(xs_g[:], xs[:].indirect(offs_t[:]))
+        for q in range(4):
+            nc.sync.dma_start(xs_p[32 * q : 32 * q + 4, :].bitcast(I32), xs_g[32 * q : 32 * q + 32 : 8, :].bitcast(I32))
+        for q in range(4):
+            nc.sync.dma_start(vs_raw[32 * q : 32 * q + 4, :].bitcast(I32), w3_scales[0, 4 * q : 4 * q + 4, :].bitcast(I32))
+            nc.sync.dma_start(vs_raw[32 * q + 4 : 32 * q + 8, :].bitcast(I32), w4_scales[0, 4 * q : 4 * q + 4, :].bitcast(I32))
+
+        rotate_v(0)
+        rotate_g(1)
+        gather_h(0, 0, 0, S)
+        gather_h(1, 0, 0, S)
+        nc.vector.tensor_copy(xw_g[:], xw[:].indirect(offs_t[:]))
+        rotate_g(2)
+        gather_h(0, 1, 0, S)
+        gather_h(1, 1, 0, S)
+        rotate_g(3)
+        gather_h(0, 2, 0, S)
+        gather_h(1, 2, 0, S)
+        cast_w(0)
+        gather_h(0, 3, 0, HALF)
+        gather_h(1, 3, 0, HALF)
+        quant_w(0)
+        cast_w(1)
+        gather_h(0, 3, HALF, S)
+        gather_h(1, 3, HALF, S)
+        quant_w(1)
+        nc.vector.tensor_copy(
+            v_q[:].bitcast(I32).rearrange("p t a (c i) -> p (a c) t i", i=4),
+            v_raw[:].rearrange("p a (c i t) -> p (a c) t i", t=PACK, i=4),
+        )
+        nc.vector.tensor_copy(
+            v_s[:].rearrange("p (t c i) -> p c t i", t=PACK, i=16),
+            vs_raw[:].rearrange("p (c i t) -> p c t i", t=PACK, i=16),
+        )
+
+        z_q, z_s, y_bf = {}, {}, {}
+
+        def front(c):
+            cols = slice(c * CHUNK, (c + 1) * CHUNK)
+            z_bf = held.tile([P, 2, CHUNK * PACK], BF16, name="z_bf%d" % c, tag="z%d" % c, align_bytes=64)
+            for a in range(2):
+                bank = psum_b.tile([P, PACK, CHUNK], F32, name="b%d" % a)
+                for t in range(PACK):
+                    m = slice(t * P, (t + 1) * P)
+                    nc.tensor.matmul_mx(
+                        out=bank[:, t, :], lhsT=w_q[a][:, m].bitcast(FP8X4), lhsT_scale=w_s[a][:, m],
+                        rhs=xw_g[:, cols].bitcast(FP8X4), rhs_scale=xs_p[:, cols], start=True, stop=True,
+                    )
+                nc.vector.tensor_tensor(
+                    z_bf[:, a, :].rearrange("p (c i t) -> p c t i", t=PACK, i=2),
+                    bank[:].rearrange("p t (c i) -> p c t i", i=2),
+                    got[a][:, :, cols].rearrange("p t (c i) -> p c t i", i=2),
+                    ALU.add,
+                )
+            return z_bf
+
+        def quant_z(c, z_bf):
+            z_q[c] = ring.tile([P, 2 * CHUNK], U32, name="z_q", align_bytes=64)
+            z_s[c] = ring.tile([P, 2 * CHUNK], U8, name="z_s", align_bytes=64)
+            nc.vector.quantize_mx(out=z_q[c][:].bitcast(FP8X4), scales=z_s[c][:], in_=z_bf[:].rearrange("p a n -> p (a n)"))
+
+        out_rows = out_0.rearrange("(p t) s -> p t s", t=PACK)
+
+        def back(c):
+            cols = slice(c * CHUNK, (c + 1) * CHUNK)
+            bank = psum_o.tile([P, PACK, CHUNK], F32, name="o")
+            for t in range(PACK):
+                m = slice(t * P, (t + 1) * P)
+                for a in range(2):
+                    n = slice(a * CHUNK, (a + 1) * CHUNK)
+                    nc.tensor.matmul_mx(
+                        out=bank[:, t, :], lhsT=v_q[:, t, a, :].bitcast(FP8X4), lhsT_scale=v_s[4 * a : P, m],
+                        rhs=z_q[c][:, n].bitcast(FP8X4), rhs_scale=z_s[c][:, n], start=(a == 0), stop=(a == 1),
+                    )
+            y_bf[c] = ring.tile([P, CHUNK * PACK], BF16, name="y_bf", align_bytes=64)
+            nc.scalar.copy(
+                y_bf[c][:].rearrange("p (c i t) -> p c t i", t=PACK, i=2),
+                bank[:].rearrange("p t (c i) -> p c t i", i=2),
+            )
+            y = held.tile([P, PACK, CHUNK], F32, name="y%d" % c)
+            nc.scalar.copy(y[:], bank[:])
+            nc.sync.dma_start(out_rows[:, :, cols], y[:])
+
+        def quant_y(c):
+            cols = slice(c * CHUNK, (c + 1) * CHUNK)
+            nc.vector.quantize_mx(out=y_q[:, cols].bitcast(FP8X4), scales=y_s[:, cols], in_=y_bf[c][:])
+            nc.sync.dma_start(as_words(out_1)[:, cols], y_q[:, cols].bitcast(I32))
+
+        z0 = front(0)
+        z1 = front(1)
+        quant_z(0, z0)
+        back(0)
+        z2 = front(2)
+        quant_z(1, z1)
+        back(1)
+        z3 = front(3)
+        quant_z(2, z2)
+        back(2)
+        quant_y(0)
+        quant_z(3, z3)
+        back(3)
+        quant_y(1)
+        quant_y(2)
+        quant_y(3)
+        for q in range(4):
+            nc.sync.dma_start(out_2[0, 4 * q : 4 * q + 4, :].bitcast(I32), y_s[32 * q : 32 * q + 4, :].bitcast(I32))

@@ -46,16 +46,15 @@ def tile_picked_lru8_none_po_kernel(
         hr_t = [held.tile([P, S], F32, name="hr%d" % t) for t in range(PACK)]
         hi_t = [held.tile([P, S], F32, name="hi%d" % t) for t in range(PACK)]
         w_raw = [held.tile([P, PACK, H], F32, name="w_raw%d" % a) for a in range(2)]
-        w_bf = [held.tile([P, H * PACK], BF16, name="w_bf%d" % a, align_bytes=64) for a in range(2)]
+        w_bf = [held.tile([P, H * PACK], BF16, name="w_bf%d" % a, tag="wb%d" % a, align_bytes=64) for a in range(2)]
         w_q = [held.tile([P, H], U32, name="w_q%d" % a, align_bytes=64) for a in range(2)]
         w_s = [held.tile([P, H], U8, name="w_s%d" % a, align_bytes=64) for a in range(2)]
         v_raw = held.tile([P, 2, N], I32, name="v_raw", tag="z0", align_bytes=64)
-        v_q = held.tile([P, PACK, 2, P], U32, name="v_q", align_bytes=64)
         vs_raw = held.tile([P, N], U8, name="vs_raw", tag="z1", align_bytes=64)
         v_s = held.tile([P, N], U8, name="v_s", align_bytes=64)
         win = [[held.tile([P, 2 * S], F32, name="win%d_%d" % (a, t)) for t in range(PACK)] for a in range(2)]
         got = [held.tile([P, PACK, S], F32, name="got%d" % a) for a in range(2)]
-        y_q = held.tile([P, S], U32, name="y_q", align_bytes=64)
+        y_all = held.tile([P, S * PACK], BF16, name="y_all", align_bytes=64)
         y_s = held.tile([P, S], U8, name="y_s", align_bytes=64)
 
         hr_rows = hr.rearrange("(p t) s -> p t s", t=PACK)
@@ -76,20 +75,32 @@ def tile_picked_lru8_none_po_kernel(
         def load_w(a):
             nc.sync.dma_start(w_raw[a][:], (w1, w2)[a].rearrange("(p j) c -> p j c", j=PACK))
 
+        def load_scales(a):
+            for q in range(4):
+                rows = slice(32 * q + 4 * a, 32 * q + 4 * a + 4)
+                nc.sync.dma_start(vs_raw[rows, :].bitcast(I32), (w3_scales, w4_scales)[a][0, 4 * q : 4 * q + 4, :].bitcast(I32))
+
         nc.sync.dma_start(li_t[:], li.rearrange("(p t) o -> p (t o)", t=PACK))
-        load_h(0)
+        nc.sync.dma_start(hi_t[0][:], hi_rows[:, 0, :])
         nc.sync.dma_start(xs[0:P:8, :].bitcast(I32), x_scales[0].bitcast(I32))
         nc.sync.dma_start(offs_t[:], offs)
+        nc.sync.dma_start(hr_t[0][:], hr_rows[:, 0, :])
         nc.sync.dma_start(lr_t[:], lr.rearrange("(p t) o -> p (t o)", t=PACK))
-        nc.sync.dma_start(par_t[:], par)
         load_h(1)
+        nc.sync.dma_start(par_t[:], par)
         nc.sync.dma_start(xw[:].bitcast(I32), as_words(x_words))
         load_h(2)
+        nc.vector.tensor_copy(xs_g[:], xs[:].indirect(offs_t[:]))
+        for q in range(4):
+            nc.sync.dma_start(xs_p[32 * q : 32 * q + 4, :].bitcast(I32), xs_g[32 * q : 32 * q + 32 : 8, :].bitcast(I32))
         load_h(3)
         load_w(0)
         load_w(1)
+        load_scales(0)
         nc.sync.dma_start(v_raw[:, 0, :], as_words(w3_words))
         nc.sync.dma_start(v_raw[:, 1, :], as_words(w4_words))
+        load_scales(1)
+
         def rotate_v(t):
             col = slice(t, t + 1)
             nc.scalar.activation(win[0][t][:, S:], hi_t[t][:], COPY, scale=li_t[:, col])
@@ -120,13 +131,6 @@ def tile_picked_lru8_none_po_kernel(
         def quant_w(a):
             nc.vector.quantize_mx(out=w_q[a][:].bitcast(FP8X4), scales=w_s[a][:], in_=w_bf[a][:])
 
-        nc.vector.tensor_copy(xs_g[:], xs[:].indirect(offs_t[:]))
-        for q in range(4):
-            nc.sync.dma_start(xs_p[32 * q : 32 * q + 4, :].bitcast(I32), xs_g[32 * q : 32 * q + 32 : 8, :].bitcast(I32))
-        for q in range(4):
-            nc.sync.dma_start(vs_raw[32 * q : 32 * q + 4, :].bitcast(I32), w3_scales[0, 4 * q : 4 * q + 4, :].bitcast(I32))
-            nc.sync.dma_start(vs_raw[32 * q + 4 : 32 * q + 8, :].bitcast(I32), w4_scales[0, 4 * q : 4 * q + 4, :].bitcast(I32))
-
         rotate_v(0)
         rotate_g(1)
         gather_h(0, 0, 0, S)
@@ -139,13 +143,12 @@ def tile_picked_lru8_none_po_kernel(
         gather_h(0, 2, 0, S)
         gather_h(1, 2, 0, S)
         cast_w(0)
-        gather_h(0, 3, 0, HALF)
-        gather_h(1, 3, 0, HALF)
+        gather_h(0, 3, 0, S)
         quant_w(0)
         cast_w(1)
-        gather_h(0, 3, HALF, S)
-        gather_h(1, 3, HALF, S)
+        gather_h(1, 3, 0, S)
         quant_w(1)
+        v_q = held.tile([P, PACK, 2, P], U32, name="v_q", tag="wb1", align_bytes=64)
         nc.vector.tensor_copy(
             v_q[:].bitcast(I32).rearrange("p t a (c i) -> p (a c) t i", i=4),
             v_raw[:].rearrange("p a (c i t) -> p (a c) t i", t=PACK, i=4),
@@ -155,74 +158,100 @@ def tile_picked_lru8_none_po_kernel(
             vs_raw[:].rearrange("p (c i t) -> p c t i", t=PACK, i=16),
         )
 
-        z_q, z_s, y_bf = {}, {}, {}
+        z_q, z_s = {}, {}
 
-        def front(c):
+        z_bf = {}
+
+        def add_input(c, a):
             cols = slice(c * CHUNK, (c + 1) * CHUNK)
-            z_bf = held.tile([P, 2, CHUNK * PACK], BF16, name="z_bf%d" % c, tag="z%d" % c, align_bytes=64)
-            for a in range(2):
-                bank = psum_b.tile([P, PACK, CHUNK], F32, name="b%d" % a)
-                for t in range(PACK):
-                    m = slice(t * P, (t + 1) * P)
-                    nc.tensor.matmul_mx(
-                        out=bank[:, t, :], lhsT=w_q[a][:, m].bitcast(FP8X4), lhsT_scale=w_s[a][:, m],
-                        rhs=xw_g[:, cols].bitcast(FP8X4), rhs_scale=xs_p[:, cols], start=True, stop=True,
-                    )
-                nc.vector.tensor_tensor(
-                    z_bf[:, a, :].rearrange("p (c i t) -> p c t i", t=PACK, i=2),
-                    bank[:].rearrange("p t (c i) -> p c t i", i=2),
-                    got[a][:, :, cols].rearrange("p t (c i) -> p c t i", i=2),
-                    ALU.add,
+            if a == 0:
+                z_bf[c] = held.tile([P, 2, CHUNK * PACK], BF16, name="z_bf%d" % c, tag="z%d" % (c % 2), align_bytes=64)
+                z_q[c] = ring.tile([P, 2 * CHUNK], U32, name="z_q", align_bytes=64)
+                z_s[c] = ring.tile([P, 2 * CHUNK], U8, name="z_s", align_bytes=64)
+            bank = psum_b.tile([P, PACK, CHUNK], F32, name="b%d" % a)
+            for t in range(PACK):
+                m = slice(t * P, (t + 1) * P)
+                nc.tensor.matmul_mx(
+                    out=bank[:, t, :], lhsT=w_q[a][:, m].bitcast(FP8X4), lhsT_scale=w_s[a][:, m],
+                    rhs=xw_g[:, cols].bitcast(FP8X4), rhs_scale=xs_p[:, cols], start=True, stop=True,
                 )
-            return z_bf
+            nc.vector.tensor_tensor(
+                z_bf[c][:, a, :].rearrange("p (c i t) -> p c t i", t=PACK, i=2),
+                bank[:].rearrange("p t (c i) -> p c t i", i=2),
+                got[a][:, :, cols].rearrange("p t (c i) -> p c t i", i=2),
+                ALU.add,
+            )
 
-        def quant_z(c, z_bf):
-            z_q[c] = ring.tile([P, 2 * CHUNK], U32, name="z_q", align_bytes=64)
-            z_s[c] = ring.tile([P, 2 * CHUNK], U8, name="z_s", align_bytes=64)
-            nc.vector.quantize_mx(out=z_q[c][:].bitcast(FP8X4), scales=z_s[c][:], in_=z_bf[:].rearrange("p a n -> p (a n)"))
+        def quant_z(c, first, last):
+            n = slice(first * CHUNK, last * CHUNK)
+            nc.vector.quantize_mx(
+                out=z_q[c][:, n].bitcast(FP8X4), scales=z_s[c][:, n], in_=z_bf[c][:, first:last, :].rearrange("p a n -> p (a n)")
+            )
 
         out_rows = out_0.rearrange("(p t) s -> p t s", t=PACK)
+
+        def product(c, t, a, dst):
+            m = slice(t * P, (t + 1) * P)
+            n = slice(a * CHUNK, (a + 1) * CHUNK)
+            nc.tensor.matmul_mx(
+                out=dst, lhsT=v_q[:, t, a, :].bitcast(FP8X4), lhsT_scale=v_s[4 * a : P, m],
+                rhs=z_q[c][:, n].bitcast(FP8X4), rhs_scale=z_s[c][:, n], start=(a == 0), stop=(a == 1),
+            )
 
         def back(c):
             cols = slice(c * CHUNK, (c + 1) * CHUNK)
             bank = psum_o.tile([P, PACK, CHUNK], F32, name="o")
             for t in range(PACK):
-                m = slice(t * P, (t + 1) * P)
                 for a in range(2):
-                    n = slice(a * CHUNK, (a + 1) * CHUNK)
-                    nc.tensor.matmul_mx(
-                        out=bank[:, t, :], lhsT=v_q[:, t, a, :].bitcast(FP8X4), lhsT_scale=v_s[4 * a : P, m],
-                        rhs=z_q[c][:, n].bitcast(FP8X4), rhs_scale=z_s[c][:, n], start=(a == 0), stop=(a == 1),
-                    )
-            y_bf[c] = ring.tile([P, CHUNK * PACK], BF16, name="y_bf", align_bytes=64)
+                    product(c, t, a, bank[:, t, :])
             nc.scalar.copy(
-                y_bf[c][:].rearrange("p (c i t) -> p c t i", t=PACK, i=2),
+                y_all[:, c * CHUNK * PACK : (c + 1) * CHUNK * PACK].rearrange("p (c i t) -> p c t i", t=PACK, i=2),
                 bank[:].rearrange("p t (c i) -> p c t i", i=2),
             )
             y = held.tile([P, PACK, CHUNK], F32, name="y%d" % c)
             nc.scalar.copy(y[:], bank[:])
             nc.sync.dma_start(out_rows[:, :, cols], y[:])
 
-        def quant_y(c):
+        def back_last(c):
             cols = slice(c * CHUNK, (c + 1) * CHUNK)
-            nc.vector.quantize_mx(out=y_q[:, cols].bitcast(FP8X4), scales=y_s[:, cols], in_=y_bf[c][:])
-            nc.sync.dma_start(as_words(out_1)[:, cols], y_q[:, cols].bitcast(I32))
+            quant_z(c, 0, 1)
+            add_input(c, 1)
+            banks = [psum_b.tile([P, CHUNK], F32, name="b%d" % (t % 2)) for t in range(PACK)]
+            for t in range(PACK):
+                product(c, t, 0, banks[t][:])
+            quant_z(c, 1, 2)
+            quant_y(0, 2, "z1")
+            y = held.tile([P, PACK, CHUNK], F32, name="y%d" % c)
+            for t in range(PACK):
+                product(c, t, 1, banks[t][:])
+                (nc.scalar.copy, nc.vector.tensor_copy)[t % 2](y[:, t, :], banks[t][:])
+            nc.sync.dma_start(out_rows[:, :, cols], y[:])
+            nc.vector.tensor_copy(
+                y_all[:, c * CHUNK * PACK : (c + 1) * CHUNK * PACK].rearrange("p (c i t) -> p c t i", t=PACK, i=4),
+                y[:].rearrange("p t (c i) -> p c t i", i=4),
+            )
 
-        z0 = front(0)
-        z1 = front(1)
-        quant_z(0, z0)
+        def quant_y(first, last, tag):
+            cols = slice(first * CHUNK, last * CHUNK)
+            y_q = held.tile([P, (last - first) * CHUNK], U32, name="y_q%d" % first, tag=tag, align_bytes=64)
+            nc.vector.quantize_mx(out=y_q[:].bitcast(FP8X4), scales=y_s[:, cols], in_=y_all[:, first * CHUNK * PACK : last * CHUNK * PACK])
+            nc.sync.dma_start(as_words(out_1)[:, cols], y_q[:].bitcast(I32))
+
+        add_input(0, 0)
+        add_input(0, 1)
+        add_input(1, 0)
+        quant_z(0, 0, 2)
         back(0)
-        z2 = front(2)
-        quant_z(1, z1)
+        add_input(1, 1)
+        add_input(2, 0)
+        quant_z(1, 0, 2)
         back(1)
-        z3 = front(3)
-        quant_z(2, z2)
+        add_input(2, 1)
+        add_input(3, 0)
+        quant_z(2, 0, 2)
         back(2)
-        quant_y(0)
-        quant_z(3, z3)
-        back(3)
-        quant_y(1)
-        quant_y(2)
-        quant_y(3)
+        back_last(3)
+        quant_y(2, 3, "yq2")
+        quant_y(3, 4, "yq3")
         for q in range(4):
-            nc.sync.dma_start(out_2[0, 4 * q : 4 * q + 4, :].bitcast(I32), y_s[32 * q : 32 * q + 4, :].bitcast(I32))
+            (nc.sync, nc.scalar)[q % 2].dma_start(out_2[0, 4 * q : 4 * q + 4, :].bitcast(I32), y_s[32 * q : 32 * q + 4, :].bitcast(I32))

@@ -46,10 +46,10 @@ def tile_picked_lru8_none_po_kernel(
         hr_t = [held.tile([P, S], F32, name="hr%d" % t) for t in range(PACK)]
         hi_t = [held.tile([P, S], F32, name="hi%d" % t) for t in range(PACK)]
         w_raw = [held.tile([P, PACK, H], F32, name="w_raw%d" % a) for a in range(2)]
-        w_bf = [held.tile([P, H * PACK], BF16, name="w_bf%d" % a, tag="wb%d" % a, align_bytes=64) for a in range(2)]
-        w_q = [held.tile([P, H], U32, name="w_q%d" % a, align_bytes=64) for a in range(2)]
+        w_bf = [held.tile([P, H * PACK], BF16, name="w_bf%d" % a, tag=("wb", "z0")[a], align_bytes=64) for a in range(2)]
+        w_q = {}
         w_s = [held.tile([P, H], U8, name="w_s%d" % a, align_bytes=64) for a in range(2)]
-        v_raw = held.tile([P, 2, N], I32, name="v_raw", tag="z0", align_bytes=64)
+        v_raw = held.tile([P, 2, N], I32, name="v_raw", tag="wq1", align_bytes=64)
         vs_raw = held.tile([P, N], U8, name="vs_raw", tag="z1", align_bytes=64)
         v_s = held.tile([P, N], U8, name="v_s", align_bytes=64)
         win = [[held.tile([P, 2 * S], F32, name="win%d_%d" % (a, t)) for t in range(PACK)] for a in range(2)]
@@ -88,8 +88,8 @@ def tile_picked_lru8_none_po_kernel(
         nc.sync.dma_start(lr_t[:], lr.rearrange("(p t) o -> p (t o)", t=PACK))
         load_h(1)
         nc.sync.dma_start(par_t[:], par)
-        nc.sync.dma_start(xw[:].bitcast(I32), as_words(x_words))
         load_h(2)
+        nc.sync.dma_start(xw[:].bitcast(I32), as_words(x_words))
         nc.vector.tensor_copy(xs_g[:], xs[:].indirect(offs_t[:]))
         for q in range(4):
             nc.sync.dma_start(xs_p[32 * q : 32 * q + 4, :].bitcast(I32), xs_g[32 * q : 32 * q + 32 : 8, :].bitcast(I32))
@@ -129,15 +129,16 @@ def tile_picked_lru8_none_po_kernel(
             )
 
         def quant_w(a):
+            w_q[a] = held.tile([P, H], U32, name="w_q%d" % a, tag="wq%d" % a, align_bytes=64)
             nc.vector.quantize_mx(out=w_q[a][:].bitcast(FP8X4), scales=w_s[a][:], in_=w_bf[a][:])
 
         rotate_v(0)
         rotate_g(1)
         gather_h(0, 0, 0, S)
         gather_h(1, 0, 0, S)
-        nc.vector.tensor_copy(xw_g[:], xw[:].indirect(offs_t[:]))
         rotate_g(2)
         gather_h(0, 1, 0, S)
+        nc.vector.tensor_copy(xw_g[:], xw[:].indirect(offs_t[:]))
         gather_h(1, 1, 0, S)
         rotate_g(3)
         gather_h(0, 2, 0, S)
@@ -147,8 +148,7 @@ def tile_picked_lru8_none_po_kernel(
         quant_w(0)
         cast_w(1)
         gather_h(1, 3, 0, S)
-        quant_w(1)
-        v_q = held.tile([P, PACK, 2, P], U32, name="v_q", tag="wb1", align_bytes=64)
+        v_q = held.tile([P, PACK, 2, P], U32, name="v_q", align_bytes=64)
         nc.vector.tensor_copy(
             v_q[:].bitcast(I32).rearrange("p t a (c i) -> p (a c) t i", i=4),
             v_raw[:].rearrange("p a (c i t) -> p (a c) t i", t=PACK, i=4),
@@ -157,6 +157,8 @@ def tile_picked_lru8_none_po_kernel(
             v_s[:].rearrange("p (t c i) -> p c t i", t=PACK, i=16),
             vs_raw[:].rearrange("p (c i t) -> p c t i", t=PACK, i=16),
         )
+
+        quant_w(1)
 
         z_q, z_s = {}, {}
 

@@ -27,6 +27,7 @@ def tile_picked_lru8_none_po_kernel(
     nc = tc.nc
     with ExitStack() as ctx:
         held = ctx.enter_context(tc.tile_pool(name="held", bufs=1))
+        laid = ctx.enter_context(tc.tile_pool(name="laid", bufs=1))
         ring = ctx.enter_context(tc.tile_pool(name="ring", bufs=4))
         psum_b = ctx.enter_context(tc.psum_pool(name="psum_b", bufs=3))
         psum_o = ctx.enter_context(tc.psum_pool(name="psum_o", bufs=2))
@@ -39,20 +40,20 @@ def tile_picked_lru8_none_po_kernel(
         lr_t = held.tile([P, PACK], F32, name="lr_t")
         li_t = held.tile([P, PACK], F32, name="li_t")
         xw = held.tile([P, T], U32, name="xw")
-        xs = held.tile([P, T], U8, name="xs")
+        xs = laid.tile([P, T], U8, name="xs", offset=8192 - 512)
         xw_g = held.tile([P, S], U32, name="xw_g", align_bytes=64)
         xs_g = held.tile([P, S], U8, name="xs_g", align_bytes=64)
         xs_p = held.tile([P, S], U8, name="xs_p", align_bytes=64)
-        hr_t = [held.tile([P, S], F32, name="hr%d" % t) for t in range(PACK)]
-        hi_t = [held.tile([P, S], F32, name="hi%d" % t) for t in range(PACK)]
-        w_raw = [held.tile([P, PACK, H], F32, name="w_raw%d" % a) for a in range(2)]
-        w_bf = [held.tile([P, H * PACK], BF16, name="w_bf%d" % a, tag=("wb", "z0")[a], align_bytes=64) for a in range(2)]
+        h_lo = [held.tile([P, 2 * S], F32, name="h_lo%d" % a, tag=("v", "hi01")[a]) for a in range(2)]
+        h_hi = [[held.tile([P, S], F32, name="h_hi%d_%d" % (a, t), tag="h%d_%d" % (a, t)) for t in (2, 3)] for a in range(2)]
+        hr_t = [h_lo[0][:, :S], h_lo[0][:, S:], h_hi[0][0][:], h_hi[0][1][:]]
+        hi_t = [h_lo[1][:, :S], h_lo[1][:, S:], h_hi[1][0][:], h_hi[1][1][:]]
+        raw = [held.tile([P, S], F32, name="raw%d" % a) for a in range(2)]
+        w_raw = {}
+        w_bf = [held.tile([P, H * PACK], BF16, name="w_bf%d" % a, tag=("wb", "vs")[a], align_bytes=64) for a in range(2)]
         w_q = {}
         w_s = [held.tile([P, H], U8, name="w_s%d" % a, align_bytes=64) for a in range(2)]
-        v_raw = held.tile([P, 2, N], I32, name="v_raw", tag="wq1", align_bytes=64)
-        vs_raw = held.tile([P, N], U8, name="vs_raw", tag="z1", align_bytes=64)
-        v_s = held.tile([P, N], U8, name="v_s", align_bytes=64)
-        win = [[held.tile([P, 2 * S], F32, name="win%d_%d" % (a, t)) for t in range(PACK)] for a in range(2)]
+        win = [{t: held.tile([P, 2 * S], F32, name="win%d_%d" % (a, t)) for t in (1, 2, 3)} for a in range(2)]
         got = [held.tile([P, PACK, S], F32, name="got%d" % a) for a in range(2)]
         y_all = held.tile([P, S * PACK], BF16, name="y_all", align_bytes=64)
         y_s = held.tile([P, S], U8, name="y_s", align_bytes=64)
@@ -62,17 +63,13 @@ def tile_picked_lru8_none_po_kernel(
 
         warm = held.tile([P, 1], F32, name="warm")
         warm2 = held.tile([P, 1], F32, name="warm2")
+        nc.gpsimd.memset(xs[:].bitcast(I32), 0)
         nc.vector.memset(warm[:], 0.0)
         nc.scalar.activation(warm2[:], warm[:], COPY)
-        nc.vector.memset(xs[:].bitcast(I32), 0)
-        nc.gpsimd.memset(xs_p[:].bitcast(I32), 0)
-        nc.gpsimd.memset(vs_raw[:].bitcast(I32), 0)
-
-        def load_h(t):
-            nc.sync.dma_start(hr_t[t][:], hr_rows[:, t, :])
-            nc.sync.dma_start(hi_t[t][:], hi_rows[:, t, :])
+        nc.vector.memset(xs_p[:].bitcast(I32), 0)
 
         def load_w(a):
+            w_raw[a] = laid.tile([P, PACK, H], F32, name="w_raw%d" % a, offset=(8192 + 512, 0)[a])
             nc.sync.dma_start(w_raw[a][:], (w1, w2)[a].rearrange("(p j) c -> p j c", j=PACK))
 
         def load_scales(a):
@@ -80,47 +77,47 @@ def tile_picked_lru8_none_po_kernel(
                 rows = slice(32 * q + 4 * a, 32 * q + 4 * a + 4)
                 nc.sync.dma_start(vs_raw[rows, :].bitcast(I32), (w3_scales, w4_scales)[a][0, 4 * q : 4 * q + 4, :].bitcast(I32))
 
-        nc.sync.dma_start(li_t[:], li.rearrange("(p t) o -> p (t o)", t=PACK))
-        nc.sync.dma_start(hi_t[0][:], hi_rows[:, 0, :])
-        nc.sync.dma_start(xs[0:P:8, :].bitcast(I32), x_scales[0].bitcast(I32))
         nc.sync.dma_start(offs_t[:], offs)
-        nc.sync.dma_start(hr_t[0][:], hr_rows[:, 0, :])
+        nc.sync.dma_start(hr_t[1], hr_rows[:, 1, :])
+        nc.sync.dma_start(xs[0:P:8, :].bitcast(I32), x_scales[0].bitcast(I32))
         nc.sync.dma_start(lr_t[:], lr.rearrange("(p t) o -> p (t o)", t=PACK))
-        load_h(1)
+        nc.sync.dma_start(li_t[:], li.rearrange("(p t) o -> p (t o)", t=PACK))
+        nc.sync.dma_start(hi_t[1], hi_rows[:, 1, :])
         nc.sync.dma_start(par_t[:], par)
-        load_h(2)
+        for t in (0, 2, 3):
+            nc.sync.dma_start(hr_t[t], hr_rows[:, t, :])
+            nc.sync.dma_start(hi_t[t], hi_rows[:, t, :])
         nc.sync.dma_start(xw[:].bitcast(I32), as_words(x_words))
         nc.vector.tensor_copy(xs_g[:], xs[:].indirect(offs_t[:]))
         for q in range(4):
             nc.sync.dma_start(xs_p[32 * q : 32 * q + 4, :].bitcast(I32), xs_g[32 * q : 32 * q + 32 : 8, :].bitcast(I32))
-        load_h(3)
+        vs_raw = laid.tile([P, N], U8, name="vs_raw", offset=8192)
+        nc.vector.memset(vs_raw[:].bitcast(I32), 0)
         load_w(0)
-        load_w(1)
         load_scales(0)
-        nc.sync.dma_start(v_raw[:, 0, :], as_words(w3_words))
-        nc.sync.dma_start(v_raw[:, 1, :], as_words(w4_words))
+        load_w(1)
         load_scales(1)
 
-        def rotate_v(t):
+        def rotate(t, re, im, parts, dst):
             col = slice(t, t + 1)
-            nc.scalar.activation(win[0][t][:, S:], hi_t[t][:], COPY, scale=li_t[:, col])
-            nc.scalar.activation(win[1][t][:, S:], hr_t[t][:], COPY, scale=li_t[:, col])
-            nc.vector.scalar_tensor_tensor(win[0][t][:, :S], hr_t[t][:], lr_t[:, col], win[0][t][:, S:], ALU.mult, ALU.subtract)
-            nc.vector.scalar_tensor_tensor(win[1][t][:, :S], hi_t[t][:], lr_t[:, col], win[1][t][:, S:], ALU.mult, ALU.add)
+            nc.scalar.activation(parts[0], re, COPY, scale=lr_t[:, col])
+            nc.scalar.activation(parts[1], im, COPY, scale=li_t[:, col])
+            nc.gpsimd.tensor_tensor(dst[0], parts[0], parts[1], ALU.subtract)
+            nc.scalar.activation(parts[2], im, COPY, scale=lr_t[:, col])
+            nc.scalar.activation(parts[3], re, COPY, scale=li_t[:, col])
+            nc.gpsimd.tensor_tensor(dst[1], parts[2], parts[3], ALU.add)
 
-        def rotate_g(t):
-            col = slice(t, t + 1)
+        def rotate_before(t):
             u = ring.tile([P, S], F32, name="u")
             v = ring.tile([P, S], F32, name="v")
-            nc.scalar.activation(win[0][t][:, S:], hr_t[t][:], COPY, scale=lr_t[:, col])
-            nc.scalar.activation(u[:], hi_t[t][:], COPY, scale=li_t[:, col])
-            nc.gpsimd.tensor_tensor(win[0][t][:, :S], win[0][t][:, S:], u[:], ALU.subtract)
-            nc.scalar.activation(win[1][t][:, S:], hi_t[t][:], COPY, scale=lr_t[:, col])
-            nc.scalar.activation(v[:], hr_t[t][:], COPY, scale=li_t[:, col])
-            nc.gpsimd.tensor_tensor(win[1][t][:, :S], win[1][t][:, S:], v[:], ALU.add)
+            rotate(t, hr_t[t], hi_t[t], [win[0][t][:, S:], u[:], win[1][t][:, S:], v[:]], [win[a][t][:, :S] for a in range(2)])
 
-        def gather_h(a, t, lo, hi_col):
-            nc.vector.tensor_copy(got[a][:, t, lo:hi_col], win[a][t][:].indirect(par_t[:, lo // 16 : hi_col // 16]))
+        def rotate_after(t):
+            parts = [held.tile([P, S], F32, name="part%d" % n, tag="h%d_%d" % (n % 2, 2 + n // 2)) for n in range(4)]
+            rotate(t, raw[0][:], raw[1][:], [part[:] for part in parts], [got[a][:, t, :] for a in range(2)])
+
+        def gather_h(a, t):
+            nc.vector.tensor_copy(got[a][:, t, :], win[a][t][:].indirect(par_t[:]))
 
         def cast_w(a):
             nc.scalar.copy(
@@ -132,33 +129,34 @@ def tile_picked_lru8_none_po_kernel(
             w_q[a] = held.tile([P, H], U32, name="w_q%d" % a, tag="wq%d" % a, align_bytes=64)
             nc.vector.quantize_mx(out=w_q[a][:].bitcast(FP8X4), scales=w_s[a][:], in_=w_bf[a][:])
 
-        rotate_v(0)
-        rotate_g(1)
-        gather_h(0, 0, 0, S)
-        gather_h(1, 0, 0, S)
-        rotate_g(2)
-        gather_h(0, 1, 0, S)
+        rotate_before(1)
+        for a in range(2):
+            nc.vector.tensor_copy(raw[a][:], h_lo[a][:].indirect(par_t[:]))
+        v_raw = held.tile([P, 2, N], I32, name="v_raw", tag="v")
+        nc.sync.dma_start(v_raw[:, 0, :], as_words(w3_words))
+        nc.sync.dma_start(v_raw[:, 1, :], as_words(w4_words))
+        gather_h(0, 1)
+        gather_h(1, 1)
+        for t in (2, 3):
+            rotate_before(t)
+            gather_h(0, t)
+            gather_h(1, t)
         nc.vector.tensor_copy(xw_g[:], xw[:].indirect(offs_t[:]))
-        gather_h(1, 1, 0, S)
-        rotate_g(3)
-        gather_h(0, 2, 0, S)
-        gather_h(1, 2, 0, S)
+        rotate_after(0)
         cast_w(0)
-        gather_h(0, 3, 0, S)
         quant_w(0)
         cast_w(1)
-        gather_h(1, 3, 0, S)
         v_q = held.tile([P, PACK, 2, P], U32, name="v_q", align_bytes=64)
         nc.vector.tensor_copy(
             v_q[:].bitcast(I32).rearrange("p t a (c i) -> p (a c) t i", i=4),
             v_raw[:].rearrange("p a (c i t) -> p (a c) t i", t=PACK, i=4),
         )
+        quant_w(1)
+        v_s = held.tile([P, N], U8, name="v_s", tag="vs", align_bytes=64)
         nc.vector.tensor_copy(
             v_s[:].rearrange("p (t c i) -> p c t i", t=PACK, i=16),
             vs_raw[:].rearrange("p (c i t) -> p c t i", t=PACK, i=16),
         )
-
-        quant_w(1)
 
         z_q, z_s = {}, {}
 

@@ -29,8 +29,7 @@ def tile_picked_lru8_none_po_kernel(
         held = ctx.enter_context(tc.tile_pool(name="held", bufs=1))
         laid = ctx.enter_context(tc.tile_pool(name="laid", bufs=1))
         ring = ctx.enter_context(tc.tile_pool(name="ring", bufs=4))
-        psum_b = ctx.enter_context(tc.psum_pool(name="psum_b", bufs=3))
-        psum_o = ctx.enter_context(tc.psum_pool(name="psum_o", bufs=2))
+        psum = ctx.enter_context(tc.psum_pool(name="psum", bufs=1))
 
         def as_words(packed):
             return packed[0].rearrange("p n t -> p (n t)").bitcast(I32)
@@ -40,22 +39,21 @@ def tile_picked_lru8_none_po_kernel(
         lr_t = held.tile([P, PACK], F32, name="lr_t")
         li_t = held.tile([P, PACK], F32, name="li_t")
         xw = held.tile([P, T], U32, name="xw")
-        xs = laid.tile([P, T], U8, name="xs", offset=8192 - 512)
+        xs = laid.tile([P, T], U8, name="xs", offset=24576 - 1024, align_bytes=64)
         xw_g = held.tile([P, S], U32, name="xw_g", align_bytes=64)
         xs_g = held.tile([P, S], U8, name="xs_g", align_bytes=64)
         xs_p = held.tile([P, S], U8, name="xs_p", align_bytes=64)
-        h_lo = [held.tile([P, 2 * S], F32, name="h_lo%d" % a, tag=("v", "hi01")[a]) for a in range(2)]
-        h_hi = [[held.tile([P, S], F32, name="h_hi%d_%d" % (a, t), tag="h%d_%d" % (a, t)) for t in (2, 3)] for a in range(2)]
+        h_lo = [laid.tile([P, 2 * S], F32, name="h_lo0", offset=4096, align_bytes=64), held.tile([P, 2 * S], F32, name="h_lo1")]
+        h_hi = [[held.tile([P, S], F32, name="h_hi%d_%d" % (a, t), tag="h%d_%d" % (a, t), align_bytes=64) for t in (2, 3)] for a in range(2)]
         hr_t = [h_lo[0][:, :S], h_lo[0][:, S:], h_hi[0][0][:], h_hi[0][1][:]]
         hi_t = [h_lo[1][:, :S], h_lo[1][:, S:], h_hi[1][0][:], h_hi[1][1][:]]
         raw = [held.tile([P, S], F32, name="raw%d" % a) for a in range(2)]
         w_raw = {}
-        w_bf = [held.tile([P, H * PACK], BF16, name="w_bf%d" % a, tag=("wb", "vs")[a], align_bytes=64) for a in range(2)]
+        w_bf = [laid.tile([P, H * PACK], BF16, name="w_bf%d" % a, offset=(0, 12288)[a], align_bytes=64) for a in range(2)]
         w_q = {}
         w_s = [held.tile([P, H], U8, name="w_s%d" % a, align_bytes=64) for a in range(2)]
         win = [{t: held.tile([P, 2 * S], F32, name="win%d_%d" % (a, t)) for t in (1, 2, 3)} for a in range(2)]
-        got = [held.tile([P, PACK, S], F32, name="got%d" % a) for a in range(2)]
-        y_all = held.tile([P, S * PACK], BF16, name="y_all", align_bytes=64)
+        got = [held.tile([P, PACK, S], F32, name="got%d" % a, tag="got%d" % a, align_bytes=64) for a in range(2)]
         y_s = held.tile([P, S], U8, name="y_s", align_bytes=64)
 
         hr_rows = hr.rearrange("(p t) s -> p t s", t=PACK)
@@ -67,15 +65,14 @@ def tile_picked_lru8_none_po_kernel(
         nc.vector.memset(warm[:], 0.0)
         nc.scalar.activation(warm2[:], warm[:], COPY)
         nc.vector.memset(xs_p[:].bitcast(I32), 0)
+        vs_raw = laid.tile([P, N], U8, name="vs_raw", offset=8192, align_bytes=64)
+        v_s = held.tile([P, N], U8, name="v_s", align_bytes=64)
+        nc.vector.memset(vs_raw[:].bitcast(I32), 0)
+        nc.vector.memset(v_s[:].bitcast(I32), 0)
 
         def load_w(a):
-            w_raw[a] = laid.tile([P, PACK, H], F32, name="w_raw%d" % a, offset=(8192 + 512, 0)[a])
+            w_raw[a] = laid.tile([P, PACK, H], F32, name="w_raw%d" % a, offset=(16384, 24576)[a], align_bytes=64)
             nc.sync.dma_start(w_raw[a][:], (w1, w2)[a].rearrange("(p j) c -> p j c", j=PACK))
-
-        def load_scales(a):
-            for q in range(4):
-                rows = slice(32 * q + 4 * a, 32 * q + 4 * a + 4)
-                nc.sync.dma_start(vs_raw[rows, :].bitcast(I32), (w3_scales, w4_scales)[a][0, 4 * q : 4 * q + 4, :].bitcast(I32))
 
         nc.sync.dma_start(offs_t[:], offs)
         nc.sync.dma_start(hr_t[1], hr_rows[:, 1, :])
@@ -88,15 +85,13 @@ def tile_picked_lru8_none_po_kernel(
             nc.sync.dma_start(hr_t[t], hr_rows[:, t, :])
             nc.sync.dma_start(hi_t[t], hi_rows[:, t, :])
         nc.sync.dma_start(xw[:].bitcast(I32), as_words(x_words))
+        for a in range(2):
+            nc.sync.dma_start(vs_raw[4 * a : P : 8, :].bitcast(I32), (w3_scales, w4_scales)[a][0].bitcast(I32))
         nc.vector.tensor_copy(xs_g[:], xs[:].indirect(offs_t[:]))
         for q in range(4):
             nc.sync.dma_start(xs_p[32 * q : 32 * q + 4, :].bitcast(I32), xs_g[32 * q : 32 * q + 32 : 8, :].bitcast(I32))
-        vs_raw = laid.tile([P, N], U8, name="vs_raw", offset=8192)
-        nc.vector.memset(vs_raw[:].bitcast(I32), 0)
         load_w(0)
-        load_scales(0)
         load_w(1)
-        load_scales(1)
 
         def rotate(t, re, im, parts, dst):
             col = slice(t, t + 1)
@@ -112,9 +107,11 @@ def tile_picked_lru8_none_po_kernel(
             v = ring.tile([P, S], F32, name="v")
             rotate(t, hr_t[t], hi_t[t], [win[0][t][:, S:], u[:], win[1][t][:, S:], v[:]], [win[a][t][:, :S] for a in range(2)])
 
-        def rotate_after(t):
-            parts = [held.tile([P, S], F32, name="part%d" % n, tag="h%d_%d" % (n % 2, 2 + n // 2)) for n in range(4)]
-            rotate(t, raw[0][:], raw[1][:], [part[:] for part in parts], [got[a][:, t, :] for a in range(2)])
+        def rotate_after(t, a, first, second):
+            col = slice(t, t + 1)
+            nc.scalar.activation(first[:], raw[a][:], COPY, scale=lr_t[:, col])
+            nc.scalar.activation(second[:], raw[1 - a][:], COPY, scale=li_t[:, col])
+            nc.gpsimd.tensor_tensor(got[a][:, t, :], first[:], second[:], (ALU.subtract, ALU.add)[a])
 
         def gather_h(a, t):
             nc.vector.tensor_copy(got[a][:, t, :], win[a][t][:].indirect(par_t[:]))
@@ -132,7 +129,7 @@ def tile_picked_lru8_none_po_kernel(
         rotate_before(1)
         for a in range(2):
             nc.vector.tensor_copy(raw[a][:], h_lo[a][:].indirect(par_t[:]))
-        v_raw = held.tile([P, 2, N], I32, name="v_raw", tag="v")
+        v_raw = laid.tile([P, 2, N], I32, name="v_raw", offset=4096, align_bytes=64)
         nc.sync.dma_start(v_raw[:, 0, :], as_words(w3_words))
         nc.sync.dma_start(v_raw[:, 1, :], as_words(w4_words))
         gather_h(0, 1)
@@ -142,7 +139,8 @@ def tile_picked_lru8_none_po_kernel(
             gather_h(0, t)
             gather_h(1, t)
         nc.vector.tensor_copy(xw_g[:], xw[:].indirect(offs_t[:]))
-        rotate_after(0)
+        rotate_after(0, 0, held.tile([P, S], F32, name="part0", tag="h0_2", align_bytes=64), held.tile([P, S], F32, name="part1", tag="h1_2", align_bytes=64))
+        rotate_after(0, 1, held.tile([P, S], F32, name="part2", tag="h0_3", align_bytes=64), held.tile([P, S], F32, name="part3", tag="h1_3", align_bytes=64))
         cast_w(0)
         quant_w(0)
         cast_w(1)
@@ -151,24 +149,28 @@ def tile_picked_lru8_none_po_kernel(
             v_q[:].bitcast(I32).rearrange("p t a (c i) -> p (a c) t i", i=4),
             v_raw[:].rearrange("p a (c i t) -> p (a c) t i", t=PACK, i=4),
         )
-        quant_w(1)
-        v_s = held.tile([P, N], U8, name="v_s", tag="vs", align_bytes=64)
+        vs_dealt = laid.tile([P, N], U8, name="vs_dealt", offset=16384, align_bytes=64)
         nc.vector.tensor_copy(
-            v_s[:].rearrange("p (t c i) -> p c t i", t=PACK, i=16),
+            vs_dealt[:].rearrange("p (t c i) -> p c t i", t=PACK, i=16),
             vs_raw[:].rearrange("p (c i t) -> p c t i", t=PACK, i=16),
         )
+        for q in range(4):
+            for a in range(2):
+                first = 32 * q + 4 * a
+                nc.sync.dma_start(v_s[first : first + 4, :].bitcast(I32), vs_dealt[first : 32 * q + 32 : 8, :].bitcast(I32))
+        w_q[1] = held.tile([P, H], U32, name="w_q1", align_bytes=64)
+        nc.vector.quantize_mx(out=w_q[1][:].bitcast(FP8X4), scales=w_s[1][:], in_=w_bf[1][:])
 
-        z_q, z_s = {}, {}
+        z_s = {}
 
         z_bf = {}
 
         def add_input(c, a):
             cols = slice(c * CHUNK, (c + 1) * CHUNK)
             if a == 0:
-                z_bf[c] = held.tile([P, 2, CHUNK * PACK], BF16, name="z_bf%d" % c, tag="z%d" % (c % 2), align_bytes=64)
-                z_q[c] = ring.tile([P, 2 * CHUNK], U32, name="z_q", align_bytes=64)
-                z_s[c] = ring.tile([P, 2 * CHUNK], U8, name="z_s", align_bytes=64)
-            bank = psum_b.tile([P, PACK, CHUNK], F32, name="b%d" % a)
+                z_bf[c] = laid.tile([P, 2, CHUNK * PACK], BF16, name="z_bf%d" % c, offset=(28672, 30720)[c % 2], align_bytes=64)
+                z_s[c] = held.tile([P, 2 * CHUNK], U8, name="z_s%d" % c, align_bytes=64)
+            bank = psum.tile([P, PACK, CHUNK], F32, name="b%d_%d" % (c, a), tag="bank%d" % ((0, 1, 2, 0), (3, 4, 5, 1))[a][c])
             for t in range(PACK):
                 m = slice(t * P, (t + 1) * P)
                 nc.tensor.matmul_mx(
@@ -200,58 +202,63 @@ def tile_picked_lru8_none_po_kernel(
 
         def back(c):
             cols = slice(c * CHUNK, (c + 1) * CHUNK)
-            bank = psum_o.tile([P, PACK, CHUNK], F32, name="o")
+            bank = psum.tile([P, PACK, CHUNK], F32, name="o%d" % c, tag="bank%d" % (6, 7, 3)[c])
             for t in range(PACK):
                 for a in range(2):
                     product(c, t, a, bank[:, t, :])
-            nc.scalar.copy(
-                y_all[:, c * CHUNK * PACK : (c + 1) * CHUNK * PACK].rearrange("p (c i t) -> p c t i", t=PACK, i=2),
-                bank[:].rearrange("p t (c i) -> p c t i", i=2),
-            )
             y = held.tile([P, PACK, CHUNK], F32, name="y%d" % c)
             nc.scalar.copy(y[:], bank[:])
             nc.sync.dma_start(out_rows[:, :, cols], y[:])
+            return bank
 
-        def back_last(c):
-            cols = slice(c * CHUNK, (c + 1) * CHUNK)
-            quant_z(c, 0, 1)
-            add_input(c, 1)
-            banks = [psum_b.tile([P, CHUNK], F32, name="b%d" % (t % 2)) for t in range(PACK)]
-            for t in range(PACK):
-                product(c, t, 0, banks[t][:])
-            quant_z(c, 1, 2)
-            quant_y(0, 2, "z1")
-            y = held.tile([P, PACK, CHUNK], F32, name="y%d" % c)
-            for t in range(PACK):
-                product(c, t, 1, banks[t][:])
-                (nc.scalar.copy, nc.vector.tensor_copy)[t % 2](y[:, t, :], banks[t][:])
-            nc.sync.dma_start(out_rows[:, :, cols], y[:])
-            nc.vector.tensor_copy(
-                y_all[:, c * CHUNK * PACK : (c + 1) * CHUNK * PACK].rearrange("p (c i t) -> p c t i", t=PACK, i=4),
-                y[:].rearrange("p t (c i) -> p c t i", i=4),
+        def round_bank(bank, y_bf, half):
+            nc.scalar.copy(
+                y_bf[:, half, :].rearrange("p (c i t) -> p c t i", t=PACK, i=2),
+                bank[:].rearrange("p t (c i) -> p c t i", i=2),
             )
 
-        def quant_y(first, last, tag):
-            cols = slice(first * CHUNK, last * CHUNK)
-            y_q = held.tile([P, (last - first) * CHUNK], U32, name="y_q%d" % first, tag=tag, align_bytes=64)
-            nc.vector.quantize_mx(out=y_q[:].bitcast(FP8X4), scales=y_s[:, cols], in_=y_all[:, first * CHUNK * PACK : last * CHUNK * PACK])
+        def quant_y(y_bf, pair, tag):
+            cols = slice(2 * pair * CHUNK, 2 * (pair + 1) * CHUNK)
+            y_q = held.tile([P, 2 * CHUNK], U32, name="y_q%d" % pair, tag=tag, align_bytes=64)
+            nc.vector.quantize_mx(out=y_q[:].bitcast(FP8X4), scales=y_s[:, cols], in_=y_bf[:].rearrange("p h n -> p (h n)"))
             nc.sync.dma_start(as_words(out_1)[:, cols], y_q[:].bitcast(I32))
 
+        z_q = [held.tile([P, 2 * CHUNK], U32, name="z_q%d" % c, tag="zq%d" % c, align_bytes=64) for c in range(4)]
+        y_bf01 = held.tile([P, 2, CHUNK * PACK], BF16, name="y_bf01", align_bytes=64)
         add_input(0, 0)
         add_input(0, 1)
         add_input(1, 0)
         quant_z(0, 0, 2)
-        back(0)
+        round_bank(back(0), y_bf01, 0)
         add_input(1, 1)
         add_input(2, 0)
         quant_z(1, 0, 2)
-        back(1)
+        round_bank(back(1), y_bf01, 1)
         add_input(2, 1)
         add_input(3, 0)
         quant_z(2, 0, 2)
-        back(2)
-        back_last(3)
-        quant_y(2, 3, "yq2")
-        quant_y(3, 4, "yq3")
+        bank2 = back(2)
+        last = 3
+        add_input(last, 1)
+        quant_z(last, 0, 1)
+        banks = [psum.tile([P, CHUNK], F32, name="last%d" % t, tag="bank%d" % (2, 4, 5, 0)[t]) for t in range(PACK)]
+        for t in range(PACK):
+            product(last, t, 0, banks[t][:])
+        quant_z(last, 1, 2)
+        y_q0 = laid.tile([P, 2 * CHUNK], U32, name="y_q0", offset=30720, align_bytes=64)
+        nc.vector.quantize_mx(out=y_q0[:].bitcast(FP8X4), scales=y_s[:, : 2 * CHUNK], in_=y_bf01[:].rearrange("p h n -> p (h n)"))
+        nc.sync.dma_start(as_words(out_1)[:, : 2 * CHUNK], y_q0[:].bitcast(I32))
+        y = held.tile([P, PACK, CHUNK], F32, name="y_last")
+        for t in range(PACK):
+            product(last, t, 1, banks[t][:])
+            (nc.scalar.copy, nc.vector.tensor_copy)[t % 2](y[:, t, :], banks[t][:])
+        nc.sync.dma_start(out_rows[:, :, last * CHUNK :], y[:])
+        y_bf23 = held.tile([P, 2, CHUNK * PACK], BF16, name="y_bf23", tag="zq3", align_bytes=64)
+        round_bank(bank2, y_bf23, 0)
+        nc.vector.tensor_copy(
+            y_bf23[:, 1, :].rearrange("p (c i t) -> p c t i", t=PACK, i=4),
+            y[:].rearrange("p t (c i) -> p c t i", i=4),
+        )
+        quant_y(y_bf23, 1, "yq23")
         for q in range(4):
             (nc.sync, nc.scalar)[q % 2].dma_start(out_2[0, 4 * q : 4 * q + 4, :].bitcast(I32), y_s[32 * q : 32 * q + 4, :].bitcast(I32))

@@ -61,8 +61,8 @@ def tile_picked_lru8_none_po_kernel(
 
         warm = held.tile([P, 1], F32, name="warm")
         warm2 = held.tile([P, 1], F32, name="warm2")
-        nc.gpsimd.memset(xs[:].bitcast(I32), 0)
         nc.vector.memset(warm[:], 0.0)
+        nc.vector.memset(xs[:].bitcast(I32), 0)
         nc.scalar.activation(warm2[:], warm[:], COPY)
         nc.vector.memset(xs_p[:].bitcast(I32), 0)
         vs_raw = laid.tile([P, N], U8, name="vs_raw", offset=8192, align_bytes=64)
@@ -76,9 +76,9 @@ def tile_picked_lru8_none_po_kernel(
 
         nc.sync.dma_start(offs_t[:], offs)
         nc.sync.dma_start(hr_t[1], hr_rows[:, 1, :])
-        nc.sync.dma_start(xs[0:P:8, :].bitcast(I32), x_scales[0].bitcast(I32))
         nc.sync.dma_start(lr_t[:], lr.rearrange("(p t) o -> p (t o)", t=PACK))
         nc.sync.dma_start(li_t[:], li.rearrange("(p t) o -> p (t o)", t=PACK))
+        nc.sync.dma_start(xs[0:P:8, :].bitcast(I32), x_scales[0].bitcast(I32))
         nc.sync.dma_start(hi_t[1], hi_rows[:, 1, :])
         nc.sync.dma_start(par_t[:], par)
         for t in (0, 2, 3):
@@ -161,26 +161,40 @@ def tile_picked_lru8_none_po_kernel(
         w_q[1] = held.tile([P, H], U32, name="w_q1", align_bytes=64)
         nc.vector.quantize_mx(out=w_q[1][:].bitcast(FP8X4), scales=w_s[1][:], in_=w_bf[1][:])
 
-        z_s = {}
+        z_bf = [laid.tile([P, 2, CHUNK * PACK], BF16, name="z_bf%d" % c, offset=(28672, 30720)[c], align_bytes=64) for c in range(2)]
+        z_s = [held.tile([P, 2 * CHUNK], U8, name="z_s%d" % c, align_bytes=64) for c in range(4)]
 
-        z_bf = {}
-
-        def add_input(c, a):
+        def project(c, a):
             cols = slice(c * CHUNK, (c + 1) * CHUNK)
-            if a == 0:
-                z_bf[c] = laid.tile([P, 2, CHUNK * PACK], BF16, name="z_bf%d" % c, offset=(28672, 30720)[c % 2], align_bytes=64)
-                z_s[c] = held.tile([P, 2 * CHUNK], U8, name="z_s%d" % c, align_bytes=64)
-            bank = psum.tile([P, PACK, CHUNK], F32, name="b%d_%d" % (c, a), tag="bank%d" % ((0, 1, 2, 0), (3, 4, 5, 1))[a][c])
+            bank = psum.tile([P, PACK, CHUNK], F32, name="b%d_%d" % (c, a), tag="bank%d" % ((0, 1, 2, 0), (3, 4, 1, 5))[a][c])
             for t in range(PACK):
                 m = slice(t * P, (t + 1) * P)
                 nc.tensor.matmul_mx(
                     out=bank[:, t, :], lhsT=w_q[a][:, m].bitcast(FP8X4), lhsT_scale=w_s[a][:, m],
                     rhs=xw_g[:, cols].bitcast(FP8X4), rhs_scale=xs_p[:, cols], start=True, stop=True,
                 )
+            return bank
+
+        def add_input(c, a):
+            cols = slice(c * CHUNK, (c + 1) * CHUNK)
             nc.vector.tensor_tensor(
                 z_bf[c][:, a, :].rearrange("p (c i t) -> p c t i", t=PACK, i=2),
-                bank[:].rearrange("p t (c i) -> p c t i", i=2),
+                project(c, a)[:].rearrange("p t (c i) -> p c t i", i=2),
                 got[a][:, :, cols].rearrange("p t (c i) -> p c t i", i=2),
+                ALU.add,
+            )
+
+        def add_input_aside(c, a):
+            cols = slice(c * CHUNK, (c + 1) * CHUNK)
+            staged = laid.tile([P, CHUNK * PACK], F32, name="staged", offset=26624, align_bytes=64)
+            nc.scalar.copy(
+                staged[:].rearrange("p (c i t) -> p c t i", t=PACK, i=2),
+                project(c, a)[:].rearrange("p t (c i) -> p c t i", i=2),
+            )
+            nc.gpsimd.tensor_tensor(
+                z_bf[c][:, a, :].rearrange("p (c t) -> p c t", t=PACK),
+                staged[:].rearrange("p (c t) -> p c t", t=PACK),
+                got[a][:, :, cols].rearrange("p t c -> p c t"),
                 ALU.add,
             )
 
@@ -202,7 +216,7 @@ def tile_picked_lru8_none_po_kernel(
 
         def back(c):
             cols = slice(c * CHUNK, (c + 1) * CHUNK)
-            bank = psum.tile([P, PACK, CHUNK], F32, name="o%d" % c, tag="bank%d" % (6, 7, 3)[c])
+            bank = psum.tile([P, PACK, CHUNK], F32, name="o%d" % c, tag="bank%d" % (6, 7)[c])
             for t in range(PACK):
                 for a in range(2):
                     product(c, t, a, bank[:, t, :])
@@ -217,48 +231,57 @@ def tile_picked_lru8_none_po_kernel(
                 bank[:].rearrange("p t (c i) -> p c t i", i=2),
             )
 
-        def quant_y(y_bf, pair, tag):
+        def round_rows(y, y_bf):
+            nc.vector.tensor_copy(
+                y_bf.rearrange("p (c i t) -> p c t i", t=PACK, i=4),
+                y[:].rearrange("p t (c i) -> p c t i", i=4),
+            )
+
+        def quant_y(y_bf, pair):
             cols = slice(2 * pair * CHUNK, 2 * (pair + 1) * CHUNK)
-            y_q = held.tile([P, 2 * CHUNK], U32, name="y_q%d" % pair, tag=tag, align_bytes=64)
+            y_q = held.tile([P, 2 * CHUNK], U32, name="y_q%d" % pair, align_bytes=64)
             nc.vector.quantize_mx(out=y_q[:].bitcast(FP8X4), scales=y_s[:, cols], in_=y_bf[:].rearrange("p h n -> p (h n)"))
             nc.sync.dma_start(as_words(out_1)[:, cols], y_q[:].bitcast(I32))
 
-        z_q = [held.tile([P, 2 * CHUNK], U32, name="z_q%d" % c, tag="zq%d" % c, align_bytes=64) for c in range(4)]
+        z_q = [held.tile([P, 2 * CHUNK], U32, name="z_q%d" % c, align_bytes=64) for c in range(4)]
         y_bf01 = held.tile([P, 2, CHUNK * PACK], BF16, name="y_bf01", align_bytes=64)
+        y_bf23 = held.tile([P, 2, CHUNK * PACK], BF16, name="y_bf23", align_bytes=64)
+        z_bf.append(laid.tile([P, 2, CHUNK * PACK], BF16, name="z_bf2", offset=12288, align_bytes=64))
+        add_input_aside(2, 0)
         add_input(0, 0)
         add_input(0, 1)
         add_input(1, 0)
         quant_z(0, 0, 2)
+        z_bf.append(laid.tile([P, 2, CHUNK * PACK], BF16, name="z_bf3", offset=28672, align_bytes=64))
         round_bank(back(0), y_bf01, 0)
         add_input(1, 1)
-        add_input(2, 0)
+        quant_z(2, 0, 1)
+        add_input(3, 0)
         quant_z(1, 0, 2)
         round_bank(back(1), y_bf01, 1)
+        banks = [psum.tile([P, CHUNK], F32, name="split%d" % t, tag="bank%d" % (2, 3, 4, 0)[t]) for t in range(PACK)]
+        for t in range(PACK):
+            product(2, t, 0, banks[t][:])
         add_input(2, 1)
-        add_input(3, 0)
-        quant_z(2, 0, 2)
-        bank2 = back(2)
-        last = 3
-        add_input(last, 1)
-        quant_z(last, 0, 1)
-        banks = [psum.tile([P, CHUNK], F32, name="last%d" % t, tag="bank%d" % (2, 4, 5, 0)[t]) for t in range(PACK)]
+        add_input(3, 1)
+        quant_z(2, 1, 2)
+        quant_z(3, 0, 2)
+        y2 = held.tile([P, PACK, CHUNK], F32, name="y_split")
         for t in range(PACK):
-            product(last, t, 0, banks[t][:])
-        quant_z(last, 1, 2)
-        y_q0 = laid.tile([P, 2 * CHUNK], U32, name="y_q0", offset=30720, align_bytes=64)
-        nc.vector.quantize_mx(out=y_q0[:].bitcast(FP8X4), scales=y_s[:, : 2 * CHUNK], in_=y_bf01[:].rearrange("p h n -> p (h n)"))
-        nc.sync.dma_start(as_words(out_1)[:, : 2 * CHUNK], y_q0[:].bitcast(I32))
-        y = held.tile([P, PACK, CHUNK], F32, name="y_last")
-        for t in range(PACK):
-            product(last, t, 1, banks[t][:])
-            (nc.scalar.copy, nc.vector.tensor_copy)[t % 2](y[:, t, :], banks[t][:])
-        nc.sync.dma_start(out_rows[:, :, last * CHUNK :], y[:])
-        y_bf23 = held.tile([P, 2, CHUNK * PACK], BF16, name="y_bf23", tag="zq3", align_bytes=64)
-        round_bank(bank2, y_bf23, 0)
-        nc.vector.tensor_copy(
-            y_bf23[:, 1, :].rearrange("p (c i t) -> p c t i", t=PACK, i=4),
-            y[:].rearrange("p t (c i) -> p c t i", i=4),
-        )
-        quant_y(y_bf23, 1, "yq23")
+            product(2, t, 1, banks[t][:])
+            (nc.scalar.copy, nc.vector.tensor_copy)[t % 2](y2[:, t, :], banks[t][:])
+        nc.sync.dma_start(out_rows[:, :, 2 * CHUNK : 3 * CHUNK], y2[:])
+        y3 = held.tile([P, PACK, CHUNK], F32, name="y_last")
+        for half in range(2):
+            bank = psum.tile([P, 2, CHUNK], F32, name="last%d" % half, tag="bank%d" % (1, 5)[half])
+            for n in range(2):
+                for a in range(2):
+                    product(3, 2 * half + n, a, bank[:, n, :])
+            nc.scalar.copy(y3[:, 2 * half : 2 * half + 2, :], bank[:])
+        nc.sync.dma_start(out_rows[:, :, 3 * CHUNK :], y3[:])
+        quant_y(y_bf01, 0)
+        round_rows(y2, y_bf23[:, 0, :])
+        round_rows(y3, y_bf23[:, 1, :])
+        quant_y(y_bf23, 1)
         for q in range(4):
             (nc.sync, nc.scalar)[q % 2].dma_start(out_2[0, 4 * q : 4 * q + 4, :].bitcast(I32), y_s[32 * q : 32 * q + 4, :].bitcast(I32))

@@ -2,7 +2,7 @@ from contextlib import ExitStack
 
 import concourse.mybir as mybir
 
-K, T, S, N, H = 512, 2048, 512, 512, 512
+T, S, N, H = 2048, 512, 512, 512
 FLOPS = 4 * 2 * 512 * 512 * 512
 
 F32 = mybir.dt.float32
@@ -17,8 +17,25 @@ COPY = mybir.ActivationFunctionType.Copy
 
 P = 128
 PACK = 4
+QUADS = 4
 CHUNK = 128
-HALF = 256
+
+AT_W_BF = (0, 12288)
+AT_HR01 = 4096
+AT_VS_RAW = 8192
+AT_W_RAW = (16384, 24576)
+AT_XS = AT_W_RAW[1] - 1024
+AT_VS_DEALT = AT_W_RAW[0]
+AT_STAGED = AT_W_RAW[1] + 2048
+AT_Z01 = (AT_W_RAW[1] + 4096, AT_W_RAW[1] + 6144)
+AT_Z2 = AT_W_BF[1]
+AT_SUMMED = AT_W_BF[1] + 2048
+AT_Z3 = AT_Z01[0]
+
+BANK_IN = ((0, 1, 2, 0), (3, 4, 1, 5))
+BANK_OUT = (6, 7)
+BANK_OUT2 = (2, 3, 4, 0)
+BANK_OUT3 = (1, 5)
 
 
 def tile_picked_lru8_none_po_kernel(
@@ -39,17 +56,17 @@ def tile_picked_lru8_none_po_kernel(
         lr_t = held.tile([P, PACK], F32, name="lr_t")
         li_t = held.tile([P, PACK], F32, name="li_t")
         xw = held.tile([P, T], U32, name="xw")
-        xs = laid.tile([P, T], U8, name="xs", offset=24576 - 1024, align_bytes=64)
+        xs = laid.tile([P, T], U8, name="xs", offset=AT_XS, align_bytes=64)
         xw_g = held.tile([P, S], U32, name="xw_g", align_bytes=64)
         xs_g = held.tile([P, S], U8, name="xs_g", align_bytes=64)
         xs_p = held.tile([P, S], U8, name="xs_p", align_bytes=64)
-        h_lo = [laid.tile([P, 2 * S], F32, name="h_lo0", offset=4096, align_bytes=64), held.tile([P, 2 * S], F32, name="h_lo1")]
+        h_lo = [laid.tile([P, 2 * S], F32, name="h_lo0", offset=AT_HR01, align_bytes=64), held.tile([P, 2 * S], F32, name="h_lo1")]
         h_hi = [[held.tile([P, S], F32, name="h_hi%d_%d" % (a, t), tag="h%d_%d" % (a, t), align_bytes=64) for t in (2, 3)] for a in range(2)]
         hr_t = [h_lo[0][:, :S], h_lo[0][:, S:], h_hi[0][0][:], h_hi[0][1][:]]
         hi_t = [h_lo[1][:, :S], h_lo[1][:, S:], h_hi[1][0][:], h_hi[1][1][:]]
         raw = [held.tile([P, S], F32, name="raw%d" % a) for a in range(2)]
         w_raw = {}
-        w_bf = [laid.tile([P, H * PACK], BF16, name="w_bf%d" % a, offset=(0, 12288)[a], align_bytes=64) for a in range(2)]
+        w_bf = [laid.tile([P, H * PACK], BF16, name="w_bf%d" % a, offset=AT_W_BF[a], align_bytes=64) for a in range(2)]
         w_q = {}
         w_s = [held.tile([P, H], U8, name="w_s%d" % a, align_bytes=64) for a in range(2)]
         win = [{t: held.tile([P, 2 * S], F32, name="win%d_%d" % (a, t)) for t in (1, 2, 3)} for a in range(2)]
@@ -59,19 +76,19 @@ def tile_picked_lru8_none_po_kernel(
         hr_rows = hr.rearrange("(p t) s -> p t s", t=PACK)
         hi_rows = hi.rearrange("(p t) s -> p t s", t=PACK)
 
-        warm = held.tile([P, 1], F32, name="warm")
-        warm2 = held.tile([P, 1], F32, name="warm2")
-        nc.vector.memset(warm[:], 0.0)
+        warm_in = held.tile([P, 1], F32, name="warm")
+        warm_out = held.tile([P, 1], F32, name="warm2")
+        nc.vector.memset(warm_in[:], 0.0)
         nc.vector.memset(xs[:].bitcast(I32), 0)
-        nc.scalar.activation(warm2[:], warm[:], COPY)
+        nc.scalar.activation(warm_out[:], warm_in[:], COPY)
         nc.vector.memset(xs_p[:].bitcast(I32), 0)
-        vs_raw = laid.tile([P, N], U8, name="vs_raw", offset=8192, align_bytes=64)
+        vs_raw = laid.tile([P, N], U8, name="vs_raw", offset=AT_VS_RAW, align_bytes=64)
         v_s = held.tile([P, N], U8, name="v_s", align_bytes=64)
         nc.vector.memset(vs_raw[:].bitcast(I32), 0)
         nc.vector.memset(v_s[:].bitcast(I32), 0)
 
         def load_w(a):
-            w_raw[a] = laid.tile([P, PACK, H], F32, name="w_raw%d" % a, offset=(16384, 24576)[a], align_bytes=64)
+            w_raw[a] = laid.tile([P, PACK, H], F32, name="w_raw%d" % a, offset=AT_W_RAW[a], align_bytes=64)
             nc.sync.dma_start(w_raw[a][:], (w1, w2)[a].rearrange("(p j) c -> p j c", j=PACK))
 
         nc.sync.dma_start(offs_t[:], offs)
@@ -88,30 +105,29 @@ def tile_picked_lru8_none_po_kernel(
         for a in range(2):
             nc.sync.dma_start(vs_raw[4 * a : P : 8, :].bitcast(I32), (w3_scales, w4_scales)[a][0].bitcast(I32))
         nc.vector.tensor_copy(xs_g[:], xs[:].indirect(offs_t[:]))
-        for q in range(4):
-            nc.sync.dma_start(xs_p[32 * q : 32 * q + 4, :].bitcast(I32), xs_g[32 * q : 32 * q + 32 : 8, :].bitcast(I32))
+        for quad in range(QUADS):
+            first = 32 * quad
+            nc.sync.dma_start(xs_p[first : first + 4, :].bitcast(I32), xs_g[first : first + 32 : 8, :].bitcast(I32))
         load_w(0)
         load_w(1)
 
-        def rotate(t, re, im, parts, dst):
-            col = slice(t, t + 1)
-            nc.scalar.activation(parts[0], re, COPY, scale=lr_t[:, col])
-            nc.scalar.activation(parts[1], im, COPY, scale=li_t[:, col])
-            nc.gpsimd.tensor_tensor(dst[0], parts[0], parts[1], ALU.subtract)
-            nc.scalar.activation(parts[2], im, COPY, scale=lr_t[:, col])
-            nc.scalar.activation(parts[3], re, COPY, scale=li_t[:, col])
-            nc.gpsimd.tensor_tensor(dst[1], parts[2], parts[3], ALU.add)
-
         def rotate_before(t):
-            u = ring.tile([P, S], F32, name="u")
-            v = ring.tile([P, S], F32, name="v")
-            rotate(t, hr_t[t], hi_t[t], [win[0][t][:, S:], u[:], win[1][t][:, S:], v[:]], [win[a][t][:, :S] for a in range(2)])
-
-        def rotate_after(t, a, first, second):
             col = slice(t, t + 1)
-            nc.scalar.activation(first[:], raw[a][:], COPY, scale=lr_t[:, col])
-            nc.scalar.activation(second[:], raw[1 - a][:], COPY, scale=li_t[:, col])
-            nc.gpsimd.tensor_tensor(got[a][:, t, :], first[:], second[:], (ALU.subtract, ALU.add)[a])
+            li_hi = ring.tile([P, S], F32, name="u")
+            li_hr = ring.tile([P, S], F32, name="v")
+            nc.scalar.activation(win[0][t][:, S:], hr_t[t], COPY, scale=lr_t[:, col])
+            nc.scalar.activation(li_hi[:], hi_t[t], COPY, scale=li_t[:, col])
+            nc.gpsimd.tensor_tensor(win[0][t][:, :S], win[0][t][:, S:], li_hi[:], ALU.subtract)
+            nc.scalar.activation(win[1][t][:, S:], hi_t[t], COPY, scale=lr_t[:, col])
+            nc.scalar.activation(li_hr[:], hr_t[t], COPY, scale=li_t[:, col])
+            nc.gpsimd.tensor_tensor(win[1][t][:, :S], win[1][t][:, S:], li_hr[:], ALU.add)
+
+        def rotate_slot0(a):
+            by_lr = held.tile([P, S], F32, name="part%d" % (2 * a), tag="h0_%d" % (2 + a), align_bytes=64)
+            by_li = held.tile([P, S], F32, name="part%d" % (2 * a + 1), tag="h1_%d" % (2 + a), align_bytes=64)
+            nc.scalar.activation(by_lr[:], raw[a][:], COPY, scale=lr_t[:, 0:1])
+            nc.scalar.activation(by_li[:], raw[1 - a][:], COPY, scale=li_t[:, 0:1])
+            nc.gpsimd.tensor_tensor(got[a][:, 0, :], by_lr[:], by_li[:], (ALU.subtract, ALU.add)[a])
 
         def gather_h(a, t):
             nc.vector.tensor_copy(got[a][:, t, :], win[a][t][:].indirect(par_t[:]))
@@ -122,14 +138,10 @@ def tile_picked_lru8_none_po_kernel(
                 w_raw[a][:].rearrange("p j (m t) -> p m j t", t=PACK),
             )
 
-        def quant_w(a):
-            w_q[a] = held.tile([P, H], U32, name="w_q%d" % a, tag="wq%d" % a, align_bytes=64)
-            nc.vector.quantize_mx(out=w_q[a][:].bitcast(FP8X4), scales=w_s[a][:], in_=w_bf[a][:])
-
         rotate_before(1)
         for a in range(2):
             nc.vector.tensor_copy(raw[a][:], h_lo[a][:].indirect(par_t[:]))
-        v_raw = laid.tile([P, 2, N], I32, name="v_raw", offset=4096, align_bytes=64)
+        v_raw = laid.tile([P, 2, N], I32, name="v_raw", offset=AT_HR01, align_bytes=64)
         nc.sync.dma_start(v_raw[:, 0, :], as_words(w3_words))
         nc.sync.dma_start(v_raw[:, 1, :], as_words(w4_words))
         gather_h(0, 1)
@@ -139,34 +151,36 @@ def tile_picked_lru8_none_po_kernel(
             gather_h(0, t)
             gather_h(1, t)
         nc.vector.tensor_copy(xw_g[:], xw[:].indirect(offs_t[:]))
-        rotate_after(0, 0, held.tile([P, S], F32, name="part0", tag="h0_2", align_bytes=64), held.tile([P, S], F32, name="part1", tag="h1_2", align_bytes=64))
-        rotate_after(0, 1, held.tile([P, S], F32, name="part2", tag="h0_3", align_bytes=64), held.tile([P, S], F32, name="part3", tag="h1_3", align_bytes=64))
+        rotate_slot0(0)
+        rotate_slot0(1)
         cast_w(0)
-        quant_w(0)
+        w_q[0] = held.tile([P, H], U32, name="w_q0", tag="wq0", align_bytes=64)
+        nc.vector.quantize_mx(out=w_q[0][:].bitcast(FP8X4), scales=w_s[0][:], in_=w_bf[0][:])
         cast_w(1)
+
         v_q = held.tile([P, PACK, 2, P], U32, name="v_q", align_bytes=64)
         nc.vector.tensor_copy(
             v_q[:].bitcast(I32).rearrange("p t a (c i) -> p (a c) t i", i=4),
             v_raw[:].rearrange("p a (c i t) -> p (a c) t i", t=PACK, i=4),
         )
-        vs_dealt = laid.tile([P, N], U8, name="vs_dealt", offset=16384, align_bytes=64)
+        vs_dealt = laid.tile([P, N], U8, name="vs_dealt", offset=AT_VS_DEALT, align_bytes=64)
         nc.vector.tensor_copy(
             vs_dealt[:].rearrange("p (t c i) -> p c t i", t=PACK, i=16),
             vs_raw[:].rearrange("p (c i t) -> p c t i", t=PACK, i=16),
         )
-        for q in range(4):
+        for quad in range(QUADS):
             for a in range(2):
-                first = 32 * q + 4 * a
-                nc.sync.dma_start(v_s[first : first + 4, :].bitcast(I32), vs_dealt[first : 32 * q + 32 : 8, :].bitcast(I32))
+                first = 32 * quad + 4 * a
+                nc.sync.dma_start(v_s[first : first + 4, :].bitcast(I32), vs_dealt[first : 32 * quad + 32 : 8, :].bitcast(I32))
         w_q[1] = held.tile([P, H], U32, name="w_q1", align_bytes=64)
         nc.vector.quantize_mx(out=w_q[1][:].bitcast(FP8X4), scales=w_s[1][:], in_=w_bf[1][:])
 
-        z_bf = [laid.tile([P, 2, CHUNK * PACK], BF16, name="z_bf%d" % c, offset=(28672, 30720)[c], align_bytes=64) for c in range(2)]
+        z_bf = [laid.tile([P, 2, CHUNK * PACK], BF16, name="z_bf%d" % c, offset=AT_Z01[c], align_bytes=64) for c in range(2)]
         z_s = [held.tile([P, 2 * CHUNK], U8, name="z_s%d" % c, align_bytes=64) for c in range(4)]
 
         def project(c, a):
             cols = slice(c * CHUNK, (c + 1) * CHUNK)
-            bank = psum.tile([P, PACK, CHUNK], F32, name="b%d_%d" % (c, a), tag="bank%d" % ((0, 1, 2, 0), (3, 4, 1, 5))[a][c])
+            bank = psum.tile([P, PACK, CHUNK], F32, name="b%d_%d" % (c, a), tag="bank%d" % BANK_IN[a][c])
             for t in range(PACK):
                 m = slice(t * P, (t + 1) * P)
                 nc.tensor.matmul_mx(
@@ -186,16 +200,13 @@ def tile_picked_lru8_none_po_kernel(
 
         def add_input_aside(c, a):
             cols = slice(c * CHUNK, (c + 1) * CHUNK)
-            staged = laid.tile([P, CHUNK * PACK], F32, name="staged", offset=26624, align_bytes=64)
+            staged = laid.tile([P, PACK, CHUNK], F32, name="staged", offset=AT_STAGED, align_bytes=64)
+            summed = laid.tile([P, PACK, CHUNK], F32, name="summed", offset=AT_SUMMED, align_bytes=64)
+            nc.scalar.copy(staged[:], project(c, a)[:])
+            nc.gpsimd.tensor_tensor(summed[:], staged[:], got[a][:, :, cols], ALU.add)
             nc.scalar.copy(
-                staged[:].rearrange("p (c i t) -> p c t i", t=PACK, i=2),
-                project(c, a)[:].rearrange("p t (c i) -> p c t i", i=2),
-            )
-            nc.gpsimd.tensor_tensor(
-                z_bf[c][:, a, :].rearrange("p (c t) -> p c t", t=PACK),
-                staged[:].rearrange("p (c t) -> p c t", t=PACK),
-                got[a][:, :, cols].rearrange("p t c -> p c t"),
-                ALU.add,
+                z_bf[c][:, a, :].rearrange("p (c i t) -> p c t i", t=PACK, i=4),
+                summed[:].rearrange("p t (c i) -> p c t i", i=4),
             )
 
         def quant_z(c, first, last):
@@ -214,20 +225,17 @@ def tile_picked_lru8_none_po_kernel(
                 rhs=z_q[c][:, n].bitcast(FP8X4), rhs_scale=z_s[c][:, n], start=(a == 0), stop=(a == 1),
             )
 
-        def back(c):
+        def finish_early(c):
             cols = slice(c * CHUNK, (c + 1) * CHUNK)
-            bank = psum.tile([P, PACK, CHUNK], F32, name="o%d" % c, tag="bank%d" % (6, 7)[c])
+            bank = psum.tile([P, PACK, CHUNK], F32, name="o%d" % c, tag="bank%d" % BANK_OUT[c])
             for t in range(PACK):
                 for a in range(2):
                     product(c, t, a, bank[:, t, :])
             y = held.tile([P, PACK, CHUNK], F32, name="y%d" % c)
             nc.scalar.copy(y[:], bank[:])
             nc.sync.dma_start(out_rows[:, :, cols], y[:])
-            return bank
-
-        def round_bank(bank, y_bf, half):
             nc.scalar.copy(
-                y_bf[:, half, :].rearrange("p (c i t) -> p c t i", t=PACK, i=2),
+                y_bf01[:, c, :].rearrange("p (c i t) -> p c t i", t=PACK, i=2),
                 bank[:].rearrange("p t (c i) -> p c t i", i=2),
             )
 
@@ -246,42 +254,45 @@ def tile_picked_lru8_none_po_kernel(
         z_q = [held.tile([P, 2 * CHUNK], U32, name="z_q%d" % c, align_bytes=64) for c in range(4)]
         y_bf01 = held.tile([P, 2, CHUNK * PACK], BF16, name="y_bf01", align_bytes=64)
         y_bf23 = held.tile([P, 2, CHUNK * PACK], BF16, name="y_bf23", align_bytes=64)
-        z_bf.append(laid.tile([P, 2, CHUNK * PACK], BF16, name="z_bf2", offset=12288, align_bytes=64))
+        z_bf.append(laid.tile([P, 2, CHUNK * PACK], BF16, name="z_bf2", offset=AT_Z2, align_bytes=64))
+
         add_input_aside(2, 0)
         add_input(0, 0)
         add_input(0, 1)
         add_input(1, 0)
         quant_z(0, 0, 2)
-        z_bf.append(laid.tile([P, 2, CHUNK * PACK], BF16, name="z_bf3", offset=28672, align_bytes=64))
-        round_bank(back(0), y_bf01, 0)
+        z_bf.append(laid.tile([P, 2, CHUNK * PACK], BF16, name="z_bf3", offset=AT_Z3, align_bytes=64))
+        finish_early(0)
         add_input(1, 1)
-        quant_z(2, 0, 1)
         add_input(3, 0)
         quant_z(1, 0, 2)
-        round_bank(back(1), y_bf01, 1)
-        banks = [psum.tile([P, CHUNK], F32, name="split%d" % t, tag="bank%d" % (2, 3, 4, 0)[t]) for t in range(PACK)]
+        finish_early(1)
+        quant_z(2, 0, 1)
+        banks2 = [psum.tile([P, CHUNK], F32, name="split%d" % t, tag="bank%d" % BANK_OUT2[t]) for t in range(PACK)]
         for t in range(PACK):
-            product(2, t, 0, banks[t][:])
+            product(2, t, 0, banks2[t][:])
         add_input(2, 1)
         add_input(3, 1)
         quant_z(2, 1, 2)
         quant_z(3, 0, 2)
         y2 = held.tile([P, PACK, CHUNK], F32, name="y_split")
         for t in range(PACK):
-            product(2, t, 1, banks[t][:])
-            (nc.scalar.copy, nc.vector.tensor_copy)[t % 2](y2[:, t, :], banks[t][:])
+            product(2, t, 1, banks2[t][:])
+            (nc.scalar.copy, nc.vector.tensor_copy)[t % 2](y2[:, t, :], banks2[t][:])
         nc.sync.dma_start(out_rows[:, :, 2 * CHUNK : 3 * CHUNK], y2[:])
         y3 = held.tile([P, PACK, CHUNK], F32, name="y_last")
         for half in range(2):
-            bank = psum.tile([P, 2, CHUNK], F32, name="last%d" % half, tag="bank%d" % (1, 5)[half])
+            bank3 = psum.tile([P, 2, CHUNK], F32, name="last%d" % half, tag="bank%d" % BANK_OUT3[half])
             for n in range(2):
                 for a in range(2):
-                    product(3, 2 * half + n, a, bank[:, n, :])
-            nc.scalar.copy(y3[:, 2 * half : 2 * half + 2, :], bank[:])
+                    product(3, 2 * half + n, a, bank3[:, n, :])
+            nc.scalar.copy(y3[:, 2 * half : 2 * half + 2, :], bank3[:])
         nc.sync.dma_start(out_rows[:, :, 3 * CHUNK :], y3[:])
         quant_y(y_bf01, 0)
         round_rows(y2, y_bf23[:, 0, :])
         round_rows(y3, y_bf23[:, 1, :])
         quant_y(y_bf23, 1)
-        for q in range(4):
-            (nc.sync, nc.scalar)[q % 2].dma_start(out_2[0, 4 * q : 4 * q + 4, :].bitcast(I32), y_s[32 * q : 32 * q + 4, :].bitcast(I32))
+        for quad in range(QUADS):
+            (nc.sync, nc.scalar)[quad % 2].dma_start(
+                out_2[0, 4 * quad : 4 * quad + 4, :].bitcast(I32), y_s[32 * quad : 32 * quad + 4, :].bitcast(I32)
+            )

@@ -64,13 +64,14 @@ def tile_picked_lru8_none_po_kernel(
         h_hi = [[held.tile([P, S], F32, name="h_hi%d_%d" % (a, t), tag="h%d_%d" % (a, t), align_bytes=64) for t in (2, 3)] for a in range(2)]
         hr_t = [h_lo[0][:, :S], h_lo[0][:, S:], h_hi[0][0][:], h_hi[0][1][:]]
         hi_t = [h_lo[1][:, :S], h_lo[1][:, S:], h_hi[1][0][:], h_hi[1][1][:]]
-        raw = [held.tile([P, S], F32, name="raw%d" % a) for a in range(2)]
         w_raw = {}
         w_bf = [laid.tile([P, H * PACK], BF16, name="w_bf%d" % a, offset=AT_W_BF[a], align_bytes=64) for a in range(2)]
         w_q = {}
         w_s = [held.tile([P, H], U8, name="w_s%d" % a, align_bytes=64) for a in range(2)]
         win = [{t: held.tile([P, 2 * S], F32, name="win%d_%d" % (a, t)) for t in (1, 2, 3)} for a in range(2)]
-        got = [held.tile([P, PACK, S], F32, name="got%d" % a, tag="got%d" % a, align_bytes=64) for a in range(2)]
+        got_flat = [held.tile([P, PACK * S], F32, name="got%d" % a, align_bytes=64) for a in range(2)]
+        got = [g[:].rearrange("p (t s) -> p t s", t=PACK) for g in got_flat]
+        raw = [held.tile([P, S], F32, name="raw_re", align_bytes=64)[:], got_flat[0][:, 3 * S :]]
         y_s = held.tile([P, S], U8, name="y_s", align_bytes=64)
 
         hr_rows = hr.rearrange("(p t) s -> p t s", t=PACK)
@@ -125,12 +126,12 @@ def tile_picked_lru8_none_po_kernel(
         def rotate_slot0(a):
             by_lr = held.tile([P, S], F32, name="part%d" % (2 * a), tag="h0_%d" % (2 + a), align_bytes=64)
             by_li = held.tile([P, S], F32, name="part%d" % (2 * a + 1), tag="h1_%d" % (2 + a), align_bytes=64)
-            nc.scalar.activation(by_lr[:], raw[a][:], COPY, scale=lr_t[:, 0:1])
-            nc.scalar.activation(by_li[:], raw[1 - a][:], COPY, scale=li_t[:, 0:1])
-            nc.gpsimd.tensor_tensor(got[a][:, 0, :], by_lr[:], by_li[:], (ALU.subtract, ALU.add)[a])
+            nc.scalar.activation(by_lr[:], raw[a], COPY, scale=lr_t[:, 0:1])
+            nc.scalar.activation(by_li[:], raw[1 - a], COPY, scale=li_t[:, 0:1])
+            nc.gpsimd.tensor_tensor(got_flat[a][:, :S], by_lr[:], by_li[:], (ALU.subtract, ALU.add)[a])
 
         def gather_h(a, t):
-            nc.vector.tensor_copy(got[a][:, t, :], win[a][t][:].indirect(par_t[:]))
+            nc.vector.tensor_copy(got_flat[a][:, t * S : (t + 1) * S], win[a][t][:].indirect(par_t[:]))
 
         def cast_w(a):
             nc.scalar.copy(
@@ -140,19 +141,21 @@ def tile_picked_lru8_none_po_kernel(
 
         rotate_before(1)
         for a in range(2):
-            nc.vector.tensor_copy(raw[a][:], h_lo[a][:].indirect(par_t[:]))
+            nc.vector.tensor_copy(raw[a], h_lo[a][:].indirect(par_t[:]))
         v_raw = laid.tile([P, 2, N], I32, name="v_raw", offset=AT_HR01, align_bytes=64)
         nc.sync.dma_start(v_raw[:, 0, :], as_words(w3_words))
         nc.sync.dma_start(v_raw[:, 1, :], as_words(w4_words))
         gather_h(0, 1)
         gather_h(1, 1)
-        for t in (2, 3):
-            rotate_before(t)
-            gather_h(0, t)
-            gather_h(1, t)
+        rotate_before(2)
+        gather_h(0, 2)
+        gather_h(1, 2)
+        rotate_before(3)
         nc.vector.tensor_copy(xw_g[:], xw[:].indirect(offs_t[:]))
         rotate_slot0(0)
         rotate_slot0(1)
+        gather_h(0, 3)
+        gather_h(1, 3)
         cast_w(0)
         w_q[0] = held.tile([P, H], U32, name="w_q0", tag="wq0", align_bytes=64)
         nc.vector.quantize_mx(out=w_q[0][:].bitcast(FP8X4), scales=w_s[0][:], in_=w_bf[0][:])

@@ -152,6 +152,13 @@ def tile_picked_lru8_none_po_kernel(
         gather_h(1, 2)
         rotate_before(3)
         nc.vector.tensor_copy(xw_g[:], xw[:].indirect(offs_t[:]))
+        idle = psum.tile([P, S], F32, name="idle", tag="bank7")
+        for n in range(4):
+            m = slice(n * P, (n + 1) * P)
+            nc.tensor.matmul_mx(
+                out=idle[:], lhsT=xw_g[:, m].bitcast(FP8X4), lhsT_scale=xs_p[:, m],
+                rhs=xw_g[:].bitcast(FP8X4), rhs_scale=xs_p[:], start=True, stop=True,
+            )
         rotate_slot0(0)
         rotate_slot0(1)
         gather_h(0, 3)

@@ -19,6 +19,7 @@ P = 128
 PACK = 4
 QUADS = 4
 CHUNK = 128
+WARM_PASSES = 4
 
 AT_W_BF = (0, 12288)
 AT_HR01 = 4096
@@ -71,7 +72,7 @@ def tile_picked_lru8_none_po_kernel(
         win = [{t: held.tile([P, 2 * S], F32, name="win%d_%d" % (a, t)) for t in (1, 2, 3)} for a in range(2)]
         got_flat = [held.tile([P, PACK * S], F32, name="got%d" % a, align_bytes=64) for a in range(2)]
         got = [g[:].rearrange("p (t s) -> p t s", t=PACK) for g in got_flat]
-        raw = [held.tile([P, S], F32, name="raw_re", align_bytes=64)[:], got_flat[0][:, 3 * S :]]
+        raw = [held.tile([P, S], F32, name="raw_re", align_bytes=64)[:], got_flat[0][:, (PACK - 1) * S :]]
         y_s = held.tile([P, S], U8, name="y_s", align_bytes=64)
 
         hr_rows = hr.rearrange("(p t) s -> p t s", t=PACK)
@@ -99,9 +100,12 @@ def tile_picked_lru8_none_po_kernel(
         nc.sync.dma_start(xs[0:P:8, :].bitcast(I32), x_scales[0].bitcast(I32))
         nc.sync.dma_start(hi_t[1], hi_rows[:, 1, :])
         nc.sync.dma_start(par_t[:], par)
-        for t in (0, 2, 3):
+        for t in (0, 2):
             nc.sync.dma_start(hr_t[t], hr_rows[:, t, :])
+        for t in (0, 2):
             nc.sync.dma_start(hi_t[t], hi_rows[:, t, :])
+        nc.sync.dma_start(hr_t[3], hr_rows[:, 3, :])
+        nc.sync.dma_start(hi_t[3], hi_rows[:, 3, :])
         nc.sync.dma_start(xw[:].bitcast(I32), as_words(x_words))
         for a in range(2):
             nc.sync.dma_start(vs_raw[4 * a : P : 8, :].bitcast(I32), (w3_scales, w4_scales)[a][0].bitcast(I32))
@@ -152,11 +156,11 @@ def tile_picked_lru8_none_po_kernel(
         gather_h(1, 2)
         rotate_before(3)
         nc.vector.tensor_copy(xw_g[:], xw[:].indirect(offs_t[:]))
-        idle = psum.tile([P, S], F32, name="idle", tag="bank7")
-        for n in range(4):
+        unread = psum.tile([P, S], F32, name="unread", tag="bank%d" % BANK_OUT[1])
+        for n in range(WARM_PASSES):
             m = slice(n * P, (n + 1) * P)
             nc.tensor.matmul_mx(
-                out=idle[:], lhsT=xw_g[:, m].bitcast(FP8X4), lhsT_scale=xs_p[:, m],
+                out=unread[:], lhsT=xw_g[:, m].bitcast(FP8X4), lhsT_scale=xs_p[:, m],
                 rhs=xw_g[:].bitcast(FP8X4), rhs_scale=xs_p[:], start=True, stop=True,
             )
         rotate_slot0(0)

@@ -139,8 +139,8 @@ def tile_picked_lru8_none_po_kernel(
 
         def cast_w(a):
             nc.scalar.copy(
-                w_bf[a][:].rearrange("p (t m j) -> p m j t", t=PACK, j=PACK),
-                w_raw[a][:].rearrange("p j (m t) -> p m j t", t=PACK),
+                w_bf[a][:].rearrange("p (t m h l) -> p m h t l", t=PACK, h=2, l=2),
+                w_raw[a][:].rearrange("p (h l) (m t) -> p m h t l", t=PACK, l=2),
             )
 
         rotate_before(1)
@@ -174,13 +174,13 @@ def tile_picked_lru8_none_po_kernel(
 
         v_q = held.tile([P, PACK, 2, P], U32, name="v_q", align_bytes=64)
         nc.vector.tensor_copy(
-            v_q[:].bitcast(I32).rearrange("p t a (c i) -> p (a c) t i", i=4),
-            v_raw[:].rearrange("p a (c i t) -> p (a c) t i", t=PACK, i=4),
+            v_q[:].bitcast(I32).rearrange("p t a (c i) -> p (a c) t i", i=2),
+            v_raw[:].rearrange("p a (c i t) -> p (a c) t i", t=PACK, i=2),
         )
         vs_dealt = laid.tile([P, N], U8, name="vs_dealt", offset=AT_VS_DEALT, align_bytes=64)
         nc.vector.tensor_copy(
-            vs_dealt[:].rearrange("p (t c i) -> p c t i", t=PACK, i=16),
-            vs_raw[:].rearrange("p (c i t) -> p c t i", t=PACK, i=16),
+            vs_dealt[:].rearrange("p (t c i) -> p c t i", t=PACK, i=8),
+            vs_raw[:].rearrange("p (c i t) -> p c t i", t=PACK, i=8),
         )
         for quad in range(QUADS):
             for a in range(2):

@@ -259,11 +259,17 @@ def tile_picked_lru8_none_po_kernel(
                 y[:].rearrange("p t (c i) -> p c t i", i=4),
             )
 
-        def quant_y(y_bf, pair):
-            cols = slice(2 * pair * CHUNK, 2 * (pair + 1) * CHUNK)
+        def quant_y(y_bf, pair, calls):
+            start = 2 * pair * CHUNK
+            width = 2 * CHUNK // calls
             y_q = held.tile([P, 2 * CHUNK], U32, name="y_q%d" % pair, align_bytes=64)
-            nc.vector.quantize_mx(out=y_q[:].bitcast(FP8X4), scales=y_s[:, cols], in_=y_bf[:].rearrange("p h n -> p (h n)"))
-            nc.sync.dma_start(as_words(out_1)[:, cols], y_q[:].bitcast(I32))
+            values = y_bf[:].rearrange("p h n -> p (h n)")
+            for n in range(0, 2 * CHUNK, width):
+                nc.vector.quantize_mx(
+                    out=y_q[:, n : n + width].bitcast(FP8X4), scales=y_s[:, start + n : start + n + width],
+                    in_=values[:, n * PACK : (n + width) * PACK],
+                )
+            nc.sync.dma_start(as_words(out_1)[:, start : start + 2 * CHUNK], y_q[:].bitcast(I32))
 
         z_q = [held.tile([P, 2 * CHUNK], U32, name="z_q%d" % c, align_bytes=64) for c in range(4)]
         y_bf01 = held.tile([P, 2, CHUNK * PACK], BF16, name="y_bf01", align_bytes=64)
@@ -302,10 +308,10 @@ def tile_picked_lru8_none_po_kernel(
                     product(3, 2 * half + n, a, bank3[:, n, :])
             nc.scalar.copy(y3[:, 2 * half : 2 * half + 2, :], bank3[:])
         nc.sync.dma_start(out_rows[:, :, 3 * CHUNK :], y3[:])
-        quant_y(y_bf01, 0)
+        quant_y(y_bf01, 0, 1)
         round_rows(y2, y_bf23[:, 0, :])
         round_rows(y3, y_bf23[:, 1, :])
-        quant_y(y_bf23, 1)
+        quant_y(y_bf23, 1, 2)
         for quad in range(QUADS):
             (nc.sync, nc.scalar)[quad % 2].dma_start(
                 out_2[0, 4 * quad : 4 * quad + 4, :].bitcast(I32), y_s[32 * quad : 32 * quad + 4, :].bitcast(I32)

@@ -19,24 +19,10 @@ P = 128
 PACK = 4
 QUADS = 4
 CHUNK = 128
-WARM_PASSES = 4
-
-AT_W_BF = (0, 12288)
-AT_HR01 = 4096
-AT_VS_RAW = 8192
-AT_W_RAW = (16384, 24576)
-AT_XS = AT_W_RAW[1] - 1024
-AT_VS_DEALT = AT_W_RAW[0]
-AT_STAGED = AT_W_RAW[1] + 2048
-AT_Z01 = (AT_W_RAW[1] + 4096, AT_W_RAW[1] + 6144)
-AT_Z2 = AT_W_BF[1]
-AT_SUMMED = AT_W_BF[1] + 2048
-AT_Z3 = AT_Z01[0]
-
-BANK_IN = ((0, 1, 2, 0), (3, 4, 1, 5))
-BANK_OUT = (6, 7)
-BANK_OUT2 = (2, 3, 4, 0)
-BANK_OUT3 = (1, 5)
+CHUNKS = S // CHUNK
+HALF = S // 2
+RE, IM = 0, 1
+BANK_OUT = (0, 2, 4, 1)
 
 
 def tile_picked_lru8_none_po_kernel(
@@ -46,7 +32,6 @@ def tile_picked_lru8_none_po_kernel(
     with ExitStack() as ctx:
         held = ctx.enter_context(tc.tile_pool(name="held", bufs=1))
         laid = ctx.enter_context(tc.tile_pool(name="laid", bufs=1))
-        ring = ctx.enter_context(tc.tile_pool(name="ring", bufs=4))
         psum = ctx.enter_context(tc.psum_pool(name="psum", bufs=1))
 
         def as_words(packed):
@@ -57,170 +42,166 @@ def tile_picked_lru8_none_po_kernel(
         lr_t = held.tile([P, PACK], F32, name="lr_t")
         li_t = held.tile([P, PACK], F32, name="li_t")
         xw = held.tile([P, T], U32, name="xw")
-        xs = laid.tile([P, T], U8, name="xs", offset=AT_XS, align_bytes=64)
+        xs = held.tile([P, T], U8, name="xs", align_bytes=64)
         xw_g = held.tile([P, S], U32, name="xw_g", align_bytes=64)
         xs_g = held.tile([P, S], U8, name="xs_g", align_bytes=64)
         xs_p = held.tile([P, S], U8, name="xs_p", align_bytes=64)
-        h_lo = [laid.tile([P, 2 * S], F32, name="h_lo0", offset=AT_HR01, align_bytes=64), held.tile([P, 2 * S], F32, name="h_lo1")]
-        h_hi = [[held.tile([P, S], F32, name="h_hi%d_%d" % (a, t), tag="h%d_%d" % (a, t), align_bytes=64) for t in (2, 3)] for a in range(2)]
-        hr_t = [h_lo[0][:, :S], h_lo[0][:, S:], h_hi[0][0][:], h_hi[0][1][:]]
-        hi_t = [h_lo[1][:, :S], h_lo[1][:, S:], h_hi[1][0][:], h_hi[1][1][:]]
-        w_raw = {}
-        w_bf = [laid.tile([P, H * PACK], BF16, name="w_bf%d" % a, offset=AT_W_BF[a], align_bytes=64) for a in range(2)]
-        w_q = {}
+        state = held.tile([P, PACK, 2, S], F32, name="state", align_bytes=64)
+        w_raw = [held.tile([P, PACK, H], F32, name="w_raw%d" % a, align_bytes=64) for a in range(2)]
+        w_q = [held.tile([P, H], U32, name="w_q%d" % a, align_bytes=64) for a in range(2)]
         w_s = [held.tile([P, H], U8, name="w_s%d" % a, align_bytes=64) for a in range(2)]
-        win = [{t: held.tile([P, 2 * S], F32, name="win%d_%d" % (a, t)) for t in (1, 2, 3)} for a in range(2)]
-        got_flat = [held.tile([P, PACK * S], F32, name="got%d" % a, align_bytes=64) for a in range(2)]
-        got = [g[:].rearrange("p (t s) -> p t s", t=PACK) for g in got_flat]
-        raw = [held.tile([P, S], F32, name="raw_re", align_bytes=64)[:], got_flat[0][:, (PACK - 1) * S :]]
+        v_raw = [laid.tile([P, N], U32, name="v_raw%d" % a, offset=16384 + 2048 * a, align_bytes=64) for a in range(2)]
+        vs_raw = held.tile([P, N], U8, name="vs_raw", align_bytes=64)
+        v_s = held.tile([P, N], U8, name="v_s", align_bytes=64)
         y_s = held.tile([P, S], U8, name="y_s", align_bytes=64)
 
-        hr_rows = hr.rearrange("(p t) s -> p t s", t=PACK)
-        hi_rows = hi.rearrange("(p t) s -> p t s", t=PACK)
+        h_rows = [h.rearrange("(p t) s -> p t s", t=PACK) for h in (hr, hi)]
+        w_rows = [w.rearrange("(p j) c -> p j c", j=PACK) for w in (w1, w2)]
 
         warm_in = held.tile([P, 1], F32, name="warm")
         warm_out = held.tile([P, 1], F32, name="warm2")
         nc.vector.memset(warm_in[:], 0.0)
-        nc.vector.memset(xs[:].bitcast(I32), 0)
         nc.scalar.activation(warm_out[:], warm_in[:], COPY)
+        nc.vector.memset(xs[:].bitcast(I32), 0)
         nc.vector.memset(xs_p[:].bitcast(I32), 0)
-        vs_raw = laid.tile([P, N], U8, name="vs_raw", offset=AT_VS_RAW, align_bytes=64)
-        v_s = held.tile([P, N], U8, name="v_s", align_bytes=64)
         nc.vector.memset(vs_raw[:].bitcast(I32), 0)
-        nc.vector.memset(v_s[:].bitcast(I32), 0)
+
+        def load_h(a, first, last):
+            nc.sync.dma_start(state[:, first:last, a, :], h_rows[a][:, first:last, :])
 
         def load_w(a):
-            w_raw[a] = laid.tile([P, PACK, H], F32, name="w_raw%d" % a, offset=AT_W_RAW[a], align_bytes=64)
-            nc.sync.dma_start(w_raw[a][:], (w1, w2)[a].rearrange("(p j) c -> p j c", j=PACK))
+            nc.sync.dma_start(w_raw[a][:], w_rows[a])
 
-        nc.sync.dma_start(offs_t[:], offs)
-        nc.sync.dma_start(hr_t[1], hr_rows[:, 1, :])
-        nc.sync.dma_start(lr_t[:], lr.rearrange("(p t) o -> p (t o)", t=PACK))
-        nc.sync.dma_start(li_t[:], li.rearrange("(p t) o -> p (t o)", t=PACK))
-        nc.sync.dma_start(xs[0:P:8, :].bitcast(I32), x_scales[0].bitcast(I32))
-        nc.sync.dma_start(hi_t[1], hi_rows[:, 1, :])
-        nc.sync.dma_start(par_t[:], par)
-        for t in (0, 2):
-            nc.sync.dma_start(hr_t[t], hr_rows[:, t, :])
-        for t in (0, 2):
-            nc.sync.dma_start(hi_t[t], hi_rows[:, t, :])
-        nc.sync.dma_start(hr_t[3], hr_rows[:, 3, :])
-        nc.sync.dma_start(hi_t[3], hi_rows[:, 3, :])
-        nc.sync.dma_start(xw[:].bitcast(I32), as_words(x_words))
-        for a in range(2):
-            nc.sync.dma_start(vs_raw[4 * a : P : 8, :].bitcast(I32), (w3_scales, w4_scales)[a][0].bitcast(I32))
-        nc.vector.tensor_copy(xs_g[:], xs[:].indirect(offs_t[:]))
-        for quad in range(QUADS):
+        def move_x_scales(quad):
             first = 32 * quad
             nc.sync.dma_start(xs_p[first : first + 4, :].bitcast(I32), xs_g[first : first + 32 : 8, :].bitcast(I32))
-        load_w(0)
-        load_w(1)
 
-        def rotate_before(t):
-            col = slice(t, t + 1)
-            li_hi = ring.tile([P, S], F32, name="u")
-            li_hr = ring.tile([P, S], F32, name="v")
-            nc.scalar.activation(win[0][t][:, S:], hr_t[t], COPY, scale=lr_t[:, col])
-            nc.scalar.activation(li_hi[:], hi_t[t], COPY, scale=li_t[:, col])
-            nc.gpsimd.tensor_tensor(win[0][t][:, :S], win[0][t][:, S:], li_hi[:], ALU.subtract)
-            nc.scalar.activation(win[1][t][:, S:], hi_t[t], COPY, scale=lr_t[:, col])
-            nc.scalar.activation(li_hr[:], hr_t[t], COPY, scale=li_t[:, col])
-            nc.gpsimd.tensor_tensor(win[1][t][:, :S], win[1][t][:, S:], li_hr[:], ALU.add)
-
-        def rotate_slot0(a):
-            by_lr = held.tile([P, S], F32, name="part%d" % (2 * a), tag="h0_%d" % (2 + a), align_bytes=64)
-            by_li = held.tile([P, S], F32, name="part%d" % (2 * a + 1), tag="h1_%d" % (2 + a), align_bytes=64)
-            nc.scalar.activation(by_lr[:], raw[a], COPY, scale=lr_t[:, 0:1])
-            nc.scalar.activation(by_li[:], raw[1 - a], COPY, scale=li_t[:, 0:1])
-            nc.gpsimd.tensor_tensor(got_flat[a][:, :S], by_lr[:], by_li[:], (ALU.subtract, ALU.add)[a])
-
-        def gather_h(a, t):
-            nc.vector.tensor_copy(got_flat[a][:, t * S : (t + 1) * S], win[a][t][:].indirect(par_t[:]))
-
-        def cast_w(a):
-            nc.scalar.copy(
-                w_bf[a][:].rearrange("p (t m h l) -> p m h t l", t=PACK, h=2, l=2),
-                w_raw[a][:].rearrange("p (h l) (m t) -> p m h t l", t=PACK, l=2),
+        def load_v_scales(a, quad):
+            first = 32 * quad + 4 * a
+            nc.sync.dma_start(
+                vs_raw[first : first + 4, :].bitcast(I32), (w3_scales, w4_scales)[a][0, 4 * quad : 4 * quad + 4, :].bitcast(I32)
             )
 
-        rotate_before(1)
+        nc.sync.dma_start(li_t[:], li.rearrange("(p t) o -> p (t o)", t=PACK))
+        load_h(RE, 0, 1)
+        load_h(IM, 0, 1)
+        nc.sync.dma_start(offs_t[:], offs)
+        nc.sync.dma_start(xs[0:P:8, :].bitcast(I32), x_scales[0].bitcast(I32))
+        nc.sync.dma_start(lr_t[:], lr.rearrange("(p t) o -> p (t o)", t=PACK))
+        nc.sync.dma_start(par_t[:], par)
+        load_h(RE, 1, 3)
+        load_h(IM, 1, 2)
+        load_h(IM, 2, 3)
+        load_h(RE, 3, 4)
+        load_h(IM, 3, 4)
+        for quad in range(3):
+            load_v_scales(RE, quad)
+        load_w(RE)
+        load_v_scales(RE, 3)
+        for quad in range(QUADS):
+            load_v_scales(IM, quad)
+        load_w(IM)
+        nc.sync.dma_start(xw[:].bitcast(I32), as_words(x_words))
+        nc.vector.tensor_copy(xs_g[:], xs[:].indirect(offs_t[:]))
+        for quad in range(QUADS):
+            move_x_scales(quad)
         for a in range(2):
-            nc.vector.tensor_copy(raw[a], h_lo[a][:].indirect(par_t[:]))
-        v_raw = laid.tile([P, 2, N], I32, name="v_raw", offset=AT_HR01, align_bytes=64)
-        nc.sync.dma_start(v_raw[:, 0, :], as_words(w3_words))
-        nc.sync.dma_start(v_raw[:, 1, :], as_words(w4_words))
-        gather_h(0, 1)
-        gather_h(1, 1)
-        rotate_before(2)
-        gather_h(0, 2)
-        gather_h(1, 2)
-        rotate_before(3)
-        nc.vector.tensor_copy(xw_g[:], xw[:].indirect(offs_t[:]))
-        unread = psum.tile([P, S], F32, name="unread", tag="bank%d" % BANK_OUT[1])
-        for n in range(WARM_PASSES):
-            m = slice(n * P, (n + 1) * P)
-            nc.tensor.matmul_mx(
-                out=unread[:], lhsT=xw_g[:, m].bitcast(FP8X4), lhsT_scale=xs_p[:, m],
-                rhs=xw_g[:].bitcast(FP8X4), rhs_scale=xs_p[:], start=True, stop=True,
-            )
-        rotate_slot0(0)
-        rotate_slot0(1)
-        gather_h(0, 3)
-        gather_h(1, 3)
-        cast_w(0)
-        w_q[0] = held.tile([P, H], U32, name="w_q0", tag="wq0", align_bytes=64)
-        nc.vector.quantize_mx(out=w_q[0][:].bitcast(FP8X4), scales=w_s[0][:], in_=w_bf[0][:])
-        cast_w(1)
+            nc.sync.dma_start(v_raw[a][:].bitcast(I32), as_words((w3_words, w4_words)[a]))
 
-        v_q = held.tile([P, PACK, 2, P], U32, name="v_q", align_bytes=64)
+        rotated = {}
+
+        def rotate(t):
+            col = slice(t, t + 1)
+            if t == 1:
+                by_li = laid.tile([P, 2, S], F32, name="by_li1", offset=0, align_bytes=64)
+            else:
+                by_li = held.tile([P, 2, S], F32, name="by_li%d" % t)
+            both = state[:, t, :, :].rearrange("p a s -> p (a s)")
+            if t == 0:
+                for a in range(2):
+                    nc.gpsimd.tensor_scalar(by_li[:, a, :], state[:, t, a, :], li_t[:, col], 0.0, ALU.mult, ALU.add)
+            elif t == 2:
+                nc.scalar.activation(by_li[:].rearrange("p a s -> p (a s)"), both, COPY, scale=li_t[:, col])
+            else:
+                for a in range(2):
+                    if t == 1:
+                        nc.scalar.activation(by_li[:, a, :], state[:, t, a, :], COPY, scale=li_t[:, col])
+                    else:
+                        nc.vector.tensor_scalar(by_li[:, a, :], state[:, t, a, :], li_t[:, col], None, ALU.mult)
+            for a in (IM, RE):
+                rotated[a, t] = held.tile([P, S], F32, name="rot%d_%d" % (a, t))
+                nc.vector.scalar_tensor_tensor(
+                    rotated[a, t][:], state[:, t, a, :], lr_t[:, col], by_li[:, 1 - a, :], ALU.mult, (ALU.subtract, ALU.add)[a]
+                )
+
+        def gather_h(a, t, half):
+            src = rotated[a, t][:].indirect(par_t[:, half * HALF // 16 : (half + 1) * HALF // 16])
+            nc.scalar.activation(picked[a][half][:, t, :], src, COPY)
+
+        def round_w(a, first, last, copy):
+            w_bf = held.tile([P, (last - first) * P * PACK], BF16, name="w_bf%d_%d" % (a, first), align_bytes=64)
+            copy(
+                w_bf[:].rearrange("p (t m h l) -> p m h t l", m=P, h=2, l=2),
+                w_raw[a][:].rearrange("p (h l) (m t) -> p m h t l", t=PACK, l=2)[:, :, :, first:last, :],
+            )
+            return w_bf
+
+        def quant_w(a, first, last, w_bf):
+            n = slice(first * P, last * P)
+            nc.vector.quantize_mx(out=w_q[a][:, n].bitcast(FP8X4), scales=w_s[a][:, n], in_=w_bf[:])
+
+        for t in range(PACK):
+            rotate(t)
+        early = laid.tile([P, 3, PACK, HALF], F32, name="picked_early", offset=0, align_bytes=64)
+        picked = [[early[:, 0], early[:, 2]], [early[:, 1], None]]
+        for t in range(PACK):
+            for a in (IM, RE):
+                gather_h(a, t, 0)
+        for t in range(PACK):
+            gather_h(RE, t, 1)
         nc.vector.tensor_copy(
-            v_q[:].bitcast(I32).rearrange("p t a (c i) -> p (a c) t i", i=2),
-            v_raw[:].rearrange("p a (c i t) -> p (a c) t i", t=PACK, i=2),
-        )
-        vs_dealt = laid.tile([P, N], U8, name="vs_dealt", offset=AT_VS_DEALT, align_bytes=64)
-        nc.vector.tensor_copy(
-            vs_dealt[:].rearrange("p (t c i) -> p c t i", t=PACK, i=8),
+            v_s[:].rearrange("p (t c i) -> p c t i", t=PACK, i=8),
             vs_raw[:].rearrange("p (c i t) -> p c t i", t=PACK, i=8),
         )
-        for quad in range(QUADS):
-            for a in range(2):
-                first = 32 * quad + 4 * a
-                nc.sync.dma_start(v_s[first : first + 4, :].bitcast(I32), vs_dealt[first : 32 * quad + 32 : 8, :].bitcast(I32))
-        w_q[1] = held.tile([P, H], U32, name="w_q1", align_bytes=64)
-        nc.vector.quantize_mx(out=w_q[1][:].bitcast(FP8X4), scales=w_s[1][:], in_=w_bf[1][:])
+        for a in range(2):
+            halves = [round_w(a, first, first + 2, nc.vector.tensor_copy) for first in (0, 2)]
+            for n in range(2):
+                quant_w(a, 2 * n, 2 * n + 2, halves[n])
+        for half in range(2):
+            nc.vector.tensor_copy(
+                xw_g[:, half * HALF : (half + 1) * HALF], xw[:].indirect(offs_t[:, half * HALF // 16 : (half + 1) * HALF // 16])
+            )
+        v_q = [held.tile([P, N], U32, name="v_q%d" % a, align_bytes=64) for a in range(2)]
+        for a in range(2):
+            nc.scalar.copy(
+                v_q[a][:].rearrange("p (t c i) -> p c t i", t=PACK, i=2),
+                v_raw[a][:].rearrange("p (c i t) -> p c t i", t=PACK, i=2),
+            )
+        picked[IM][1] = laid.tile([P, PACK, HALF], F32, name="picked_late", offset=16384, align_bytes=64)[:]
+        for t in range(PACK):
+            gather_h(IM, t, 1)
 
-        z_bf = [laid.tile([P, 2, CHUNK * PACK], BF16, name="z_bf%d" % c, offset=AT_Z01[c], align_bytes=64) for c in range(2)]
-        z_s = [held.tile([P, 2 * CHUNK], U8, name="z_s%d" % c, align_bytes=64) for c in range(4)]
+        z_bf = [held.tile([P, 2, CHUNK * PACK], BF16, name="z_bf%d" % c, align_bytes=64) for c in range(CHUNKS)]
+        z_q = [held.tile([P, 2 * CHUNK], U32, name="z_q%d" % c, align_bytes=64) for c in range(CHUNKS)]
+        z_s = [held.tile([P, 2 * CHUNK], U8, name="z_s%d" % c, align_bytes=64) for c in range(CHUNKS)]
+        y_bf = [held.tile([P, 2, CHUNK * PACK], BF16, name="y_bf%d" % n, align_bytes=64) for n in range(2)]
+        y_q = [held.tile([P, 2 * CHUNK], U32, name="y_q%d" % n, align_bytes=64) for n in range(2)]
+        out_rows = out_0.rearrange("(p t) s -> p t s", t=PACK)
 
-        def project(c, a):
+        def add_input(c, a):
             cols = slice(c * CHUNK, (c + 1) * CHUNK)
-            bank = psum.tile([P, PACK, CHUNK], F32, name="b%d_%d" % (c, a), tag="bank%d" % BANK_IN[a][c])
+            bank = psum.tile([P, PACK, CHUNK], F32, name="in%d_%d" % (c, a), tag="bank%d" % (2 * c + a))
             for t in range(PACK):
                 m = slice(t * P, (t + 1) * P)
                 nc.tensor.matmul_mx(
                     out=bank[:, t, :], lhsT=w_q[a][:, m].bitcast(FP8X4), lhsT_scale=w_s[a][:, m],
                     rhs=xw_g[:, cols].bitcast(FP8X4), rhs_scale=xs_p[:, cols], start=True, stop=True,
                 )
-            return bank
-
-        def add_input(c, a):
-            cols = slice(c * CHUNK, (c + 1) * CHUNK)
             nc.vector.tensor_tensor(
                 z_bf[c][:, a, :].rearrange("p (c i t) -> p c t i", t=PACK, i=2),
-                project(c, a)[:].rearrange("p t (c i) -> p c t i", i=2),
-                got[a][:, :, cols].rearrange("p t (c i) -> p c t i", i=2),
+                bank[:].rearrange("p t (c i) -> p c t i", i=2),
+                picked[a][c // 2][:, :, c % 2 * CHUNK : (c % 2 + 1) * CHUNK].rearrange("p t (c i) -> p c t i", i=2),
                 ALU.add,
-            )
-
-        def add_input_aside(c, a):
-            cols = slice(c * CHUNK, (c + 1) * CHUNK)
-            staged = laid.tile([P, PACK, CHUNK], F32, name="staged", offset=AT_STAGED, align_bytes=64)
-            summed = laid.tile([P, PACK, CHUNK], F32, name="summed", offset=AT_SUMMED, align_bytes=64)
-            nc.scalar.copy(staged[:], project(c, a)[:])
-            nc.gpsimd.tensor_tensor(summed[:], staged[:], got[a][:, :, cols], ALU.add)
-            nc.scalar.copy(
-                z_bf[c][:, a, :].rearrange("p (c i t) -> p c t i", t=PACK, i=4),
-                summed[:].rearrange("p t (c i) -> p c t i", i=4),
             )
 
         def quant_z(c, first, last):
@@ -229,89 +210,90 @@ def tile_picked_lru8_none_po_kernel(
                 out=z_q[c][:, n].bitcast(FP8X4), scales=z_s[c][:, n], in_=z_bf[c][:, first:last, :].rearrange("p a n -> p (a n)")
             )
 
-        out_rows = out_0.rearrange("(p t) s -> p t s", t=PACK)
+        out_bank = {}
 
-        def product(c, t, a, dst):
-            m = slice(t * P, (t + 1) * P)
+        def project_out(c, a):
+            if a == RE:
+                out_bank[c] = psum.tile([P, PACK, CHUNK], F32, name="out%d" % c, tag="bank%d" % BANK_OUT[c])
             n = slice(a * CHUNK, (a + 1) * CHUNK)
-            nc.tensor.matmul_mx(
-                out=dst, lhsT=v_q[:, t, a, :].bitcast(FP8X4), lhsT_scale=v_s[4 * a : P, m],
-                rhs=z_q[c][:, n].bitcast(FP8X4), rhs_scale=z_s[c][:, n], start=(a == 0), stop=(a == 1),
-            )
-
-        def finish_early(c):
-            cols = slice(c * CHUNK, (c + 1) * CHUNK)
-            bank = psum.tile([P, PACK, CHUNK], F32, name="o%d" % c, tag="bank%d" % BANK_OUT[c])
             for t in range(PACK):
-                for a in range(2):
-                    product(c, t, a, bank[:, t, :])
-            y = held.tile([P, PACK, CHUNK], F32, name="y%d" % c)
-            nc.scalar.copy(y[:], bank[:])
-            nc.sync.dma_start(out_rows[:, :, cols], y[:])
-            nc.scalar.copy(
-                y_bf01[:, c, :].rearrange("p (c i t) -> p c t i", t=PACK, i=2),
-                bank[:].rearrange("p t (c i) -> p c t i", i=2),
-            )
-
-        def round_rows(y, y_bf):
-            nc.vector.tensor_copy(
-                y_bf.rearrange("p (c i t) -> p c t i", t=PACK, i=4),
-                y[:].rearrange("p t (c i) -> p c t i", i=4),
-            )
-
-        def quant_y(y_bf, pair, calls):
-            start = 2 * pair * CHUNK
-            width = 2 * CHUNK // calls
-            y_q = held.tile([P, 2 * CHUNK], U32, name="y_q%d" % pair, align_bytes=64)
-            values = y_bf[:].rearrange("p h n -> p (h n)")
-            for n in range(0, 2 * CHUNK, width):
-                nc.vector.quantize_mx(
-                    out=y_q[:, n : n + width].bitcast(FP8X4), scales=y_s[:, start + n : start + n + width],
-                    in_=values[:, n * PACK : (n + width) * PACK],
+                m = slice(t * P, (t + 1) * P)
+                nc.tensor.matmul_mx(
+                    out=out_bank[c][:, t, :], lhsT=v_q[a][:, m].bitcast(FP8X4), lhsT_scale=v_s[4 * a : P, m],
+                    rhs=z_q[c][:, n].bitcast(FP8X4), rhs_scale=z_s[c][:, n],
+                    start=(a == RE and t == 0), stop=(a == IM and t == PACK - 1),
                 )
-            nc.sync.dma_start(as_words(out_1)[:, start : start + 2 * CHUNK], y_q[:].bitcast(I32))
 
-        z_q = [held.tile([P, 2 * CHUNK], U32, name="z_q%d" % c, align_bytes=64) for c in range(4)]
-        y_bf01 = held.tile([P, 2, CHUNK * PACK], BF16, name="y_bf01", align_bytes=64)
-        y_bf23 = held.tile([P, 2, CHUNK * PACK], BF16, name="y_bf23", align_bytes=64)
-        z_bf.append(laid.tile([P, 2, CHUNK * PACK], BF16, name="z_bf2", offset=AT_Z2, align_bytes=64))
+        def store_y(c):
+            y = held.tile([P, PACK, CHUNK], F32, name="y%d" % c)
+            nc.scalar.copy(y[:], out_bank[c][:])
+            nc.sync.dma_start(out_rows[:, :, c * CHUNK : (c + 1) * CHUNK], y[:])
 
-        add_input_aside(2, 0)
-        add_input(0, 0)
-        add_input(0, 1)
-        add_input(1, 0)
+        def round_y(c, copy):
+            copy(
+                y_bf[c // 2][:, c % 2, :].rearrange("p (c i t) -> p c t i", t=PACK, i=2),
+                out_bank[c][:].rearrange("p t (c i) -> p c t i", i=2),
+            )
+
+        def quant_y(first, last):
+            n = slice(first % 2 * CHUNK, ((last - 1) % 2 + 1) * CHUNK)
+            nc.vector.quantize_mx(
+                out=y_q[first // 2][:, n].bitcast(FP8X4), scales=y_s[:, first * CHUNK : last * CHUNK],
+                in_=y_bf[first // 2][:, first % 2 : (last - 1) % 2 + 1, :].rearrange("p h n -> p (h n)"),
+            )
+
+        def store_words(pair):
+            nc.sync.dma_start(as_words(out_1)[:, 2 * pair * CHUNK : 2 * (pair + 1) * CHUNK], y_q[pair][:].bitcast(I32))
+
+        def finish(c):
+            project_out(c, RE)
+            project_out(c, IM)
+            store_y(c)
+            round_y(c, nc.scalar.copy)
+
+        add_input(0, RE)
+        add_input(0, IM)
+        add_input(1, RE)
         quant_z(0, 0, 2)
-        z_bf.append(laid.tile([P, 2, CHUNK * PACK], BF16, name="z_bf3", offset=AT_Z3, align_bytes=64))
-        finish_early(0)
-        add_input(1, 1)
-        add_input(3, 0)
+        finish(0)
+        add_input(1, IM)
+        add_input(2, RE)
         quant_z(1, 0, 2)
-        finish_early(1)
-        quant_z(2, 0, 1)
-        banks2 = [psum.tile([P, CHUNK], F32, name="split%d" % t, tag="bank%d" % BANK_OUT2[t]) for t in range(PACK)]
-        for t in range(PACK):
-            product(2, t, 0, banks2[t][:])
-        add_input(2, 1)
-        add_input(3, 1)
-        quant_z(2, 1, 2)
-        quant_z(3, 0, 2)
-        y2 = held.tile([P, PACK, CHUNK], F32, name="y_split")
-        for t in range(PACK):
-            product(2, t, 1, banks2[t][:])
-            (nc.scalar.copy, nc.vector.tensor_copy)[t % 2](y2[:, t, :], banks2[t][:])
-        nc.sync.dma_start(out_rows[:, :, 2 * CHUNK : 3 * CHUNK], y2[:])
-        y3 = held.tile([P, PACK, CHUNK], F32, name="y_last")
-        for half in range(2):
-            bank3 = psum.tile([P, 2, CHUNK], F32, name="last%d" % half, tag="bank%d" % BANK_OUT3[half])
-            for n in range(2):
-                for a in range(2):
-                    product(3, 2 * half + n, a, bank3[:, n, :])
-            nc.scalar.copy(y3[:, 2 * half : 2 * half + 2, :], bank3[:])
+        finish(1)
+        add_input(2, IM)
+        add_input(3, RE)
+        quant_z(2, 0, 2)
+        finish(2)
+        quant_z(3, 0, 1)
+        last = [psum.tile([P, 2, CHUNK], F32, name="last%d" % n, tag="bank%d" % (1, 3)[n]) for n in range(2)]
+
+        def project_last(a):
+            n = slice(a * CHUNK, (a + 1) * CHUNK)
+            for t in range(PACK):
+                m = slice(t * P, (t + 1) * P)
+                nc.tensor.matmul_mx(
+                    out=last[t // 2][:, t % 2, :], lhsT=v_q[a][:, m].bitcast(FP8X4), lhsT_scale=v_s[4 * a : P, m],
+                    rhs=z_q[3][:, n].bitcast(FP8X4), rhs_scale=z_s[3][:, n],
+                    start=(a == RE and t % 2 == 0), stop=(a == IM and t % 2 == 1),
+                )
+
+        project_last(RE)
+        add_input(3, IM)
+        quant_y(0, 2)
+        store_words(0)
+        quant_z(3, 1, 2)
+        project_last(IM)
+        quant_y(2, 3)
+        y3 = held.tile([P, PACK, CHUNK], F32, name="y3")
+        nc.scalar.copy(y3[:, :2, :], last[0][:])
+        nc.vector.tensor_copy(y3[:, 2:, :], last[1][:])
         nc.sync.dma_start(out_rows[:, :, 3 * CHUNK :], y3[:])
-        quant_y(y_bf01, 0, 1)
-        round_rows(y2, y_bf23[:, 0, :])
-        round_rows(y3, y_bf23[:, 1, :])
-        quant_y(y_bf23, 1, 2)
+        nc.vector.tensor_copy(
+            y_bf[1][:, 1, :].rearrange("p (c i t) -> p c t i", t=PACK, i=4),
+            y3[:].rearrange("p t (c i) -> p c t i", i=4),
+        )
+        quant_y(3, 4)
+        store_words(1)
         for quad in range(QUADS):
             (nc.sync, nc.scalar)[quad % 2].dma_start(
                 out_2[0, 4 * quad : 4 * quad + 4, :].bitcast(I32), y_s[32 * quad : 32 * quad + 4, :].bitcast(I32)

@@ -22,7 +22,8 @@ CHUNK = 128
 CHUNKS = S // CHUNK
 HALF = S // 2
 RE, IM = 0, 1
-BANK_OUT = (0, 2, 4, 1)
+BANK_IN = ((0, 1, 2, 3), (4, 5, 6, 7))
+BANK_OUT = ((0,), (1,), (2,), (3, 4))
 
 
 def tile_picked_lru8_none_po_kernel(
@@ -46,11 +47,15 @@ def tile_picked_lru8_none_po_kernel(
         xw_g = held.tile([P, S], U32, name="xw_g", align_bytes=64)
         xs_g = held.tile([P, S], U8, name="xs_g", align_bytes=64)
         xs_p = held.tile([P, S], U8, name="xs_p", align_bytes=64)
-        state = held.tile([P, PACK, 2, S], F32, name="state", align_bytes=64)
-        w_raw = [held.tile([P, PACK, H], F32, name="w_raw%d" % a, align_bytes=64) for a in range(2)]
+        h01 = [held.tile([P, 2 * S], F32, name="h01_%d" % a) for a in range(2)]
+        h2 = held.tile([P, 2, S], F32, name="h2")
+        h3 = held.tile([P, 2, S], F32, name="h3")
+        w_raw = [held.tile([P, PACK, H], F32, name="w_raw0"), laid.tile([P, PACK, H], F32, name="w_raw1", offset=0, align_bytes=64)]
+        gathered = held.tile([P, 3, PACK, HALF], F32, name="gathered", align_bytes=64)
+        picked = [[gathered[:, 0], gathered[:, 1]], [gathered[:, 2], None]]
         w_q = [held.tile([P, H], U32, name="w_q%d" % a, align_bytes=64) for a in range(2)]
         w_s = [held.tile([P, H], U8, name="w_s%d" % a, align_bytes=64) for a in range(2)]
-        v_raw = [laid.tile([P, N], U32, name="v_raw%d" % a, offset=16384 + 2048 * a, align_bytes=64) for a in range(2)]
+        v_raw = [held.tile([P, N], U32, name="v_raw%d" % a, align_bytes=64) for a in range(2)]
         vs_raw = held.tile([P, N], U8, name="vs_raw", align_bytes=64)
         v_s = held.tile([P, N], U8, name="v_s", align_bytes=64)
         y_s = held.tile([P, S], U8, name="y_s", align_bytes=64)
@@ -66,15 +71,12 @@ def tile_picked_lru8_none_po_kernel(
         nc.vector.memset(xs_p[:].bitcast(I32), 0)
         nc.vector.memset(vs_raw[:].bitcast(I32), 0)
 
-        def load_h(a, first, last):
-            nc.sync.dma_start(state[:, first:last, a, :], h_rows[a][:, first:last, :])
-
         def load_w(a):
             nc.sync.dma_start(w_raw[a][:], w_rows[a])
 
         def move_x_scales(quad):
             first = 32 * quad
-            nc.sync.dma_start(xs_p[first : first + 4, :].bitcast(I32), xs_g[first : first + 32 : 8, :].bitcast(I32))
+            nc.gpsimd.dma_start(xs_p[first : first + 4, :].bitcast(I32), xs_g[first : first + 32 : 8, :].bitcast(I32))
 
         def load_v_scales(a, quad):
             first = 32 * quad + 4 * a
@@ -82,57 +84,46 @@ def tile_picked_lru8_none_po_kernel(
                 vs_raw[first : first + 4, :].bitcast(I32), (w3_scales, w4_scales)[a][0, 4 * quad : 4 * quad + 4, :].bitcast(I32)
             )
 
+        nc.sync.dma_start(par_t[:], par)
         nc.sync.dma_start(li_t[:], li.rearrange("(p t) o -> p (t o)", t=PACK))
-        load_h(RE, 0, 1)
-        load_h(IM, 0, 1)
+        nc.sync.dma_start(h01[RE][:].rearrange("p (t s) -> p t s", t=2), h_rows[RE][:, :2, :])
         nc.sync.dma_start(offs_t[:], offs)
         nc.sync.dma_start(xs[0:P:8, :].bitcast(I32), x_scales[0].bitcast(I32))
+        nc.sync.dma_start(h01[IM][:, S:], h_rows[IM][:, 1, :])
         nc.sync.dma_start(lr_t[:], lr.rearrange("(p t) o -> p (t o)", t=PACK))
-        nc.sync.dma_start(par_t[:], par)
-        load_h(RE, 1, 3)
-        load_h(IM, 1, 2)
-        load_h(IM, 2, 3)
-        load_h(RE, 3, 4)
-        load_h(IM, 3, 4)
-        for quad in range(3):
-            load_v_scales(RE, quad)
+        nc.sync.dma_start(h01[IM][:, :S], h_rows[IM][:, 0, :])
+        for t, h_t in ((2, h2), (3, h3)):
+            for a in range(2):
+                nc.sync.dma_start(h_t[:, a, :], h_rows[a][:, t, :])
         load_w(RE)
+        load_v_scales(RE, 0)
+        load_v_scales(RE, 1)
+        nc.sync.dma_start(xw[:].bitcast(I32), as_words(x_words))
+        load_v_scales(RE, 2)
         load_v_scales(RE, 3)
         for quad in range(QUADS):
             load_v_scales(IM, quad)
         load_w(IM)
-        nc.sync.dma_start(xw[:].bitcast(I32), as_words(x_words))
-        nc.vector.tensor_copy(xs_g[:], xs[:].indirect(offs_t[:]))
-        for quad in range(QUADS):
-            move_x_scales(quad)
         for a in range(2):
             nc.sync.dma_start(v_raw[a][:].bitcast(I32), as_words((w3_words, w4_words)[a]))
+        nc.vector.tensor_copy(xs_g[:], xs[:].indirect(offs_t[:]))
+
+        def rotate(t, parts, by_li, dst):
+            for a in (IM, RE):
+                nc.vector.scalar_tensor_tensor(dst[a], parts[a], lr_t[:, t : t + 1], by_li[1 - a], ALU.mult, (ALU.subtract, ALU.add)[a])
 
         rotated = {}
 
-        def rotate(t):
-            col = slice(t, t + 1)
-            if t == 1:
-                by_li = laid.tile([P, 2, S], F32, name="by_li1", offset=0, align_bytes=64)
-            else:
-                by_li = held.tile([P, 2, S], F32, name="by_li%d" % t)
-            both = state[:, t, :, :].rearrange("p a s -> p (a s)")
-            if t == 0:
-                for a in range(2):
-                    nc.gpsimd.tensor_scalar(by_li[:, a, :], state[:, t, a, :], li_t[:, col], 0.0, ALU.mult, ALU.add)
-            elif t == 2:
-                nc.scalar.activation(by_li[:].rearrange("p a s -> p (a s)"), both, COPY, scale=li_t[:, col])
-            else:
-                for a in range(2):
-                    if t == 1:
-                        nc.scalar.activation(by_li[:, a, :], state[:, t, a, :], COPY, scale=li_t[:, col])
-                    else:
-                        nc.vector.tensor_scalar(by_li[:, a, :], state[:, t, a, :], li_t[:, col], None, ALU.mult)
-            for a in (IM, RE):
+        def rotate_before(t, parts):
+            by_li = held.tile([P, 2, S], F32, name="by_li%d" % t)
+            for a in range(2):
+                if t == 1:
+                    nc.gpsimd.tensor_scalar(by_li[:, a, :], parts[a], li_t[:, t : t + 1], 0.0, ALU.mult, ALU.add)
+                else:
+                    nc.vector.tensor_scalar(by_li[:, a, :], parts[a], li_t[:, t : t + 1], None, ALU.mult)
+            for a in range(2):
                 rotated[a, t] = held.tile([P, S], F32, name="rot%d_%d" % (a, t))
-                nc.vector.scalar_tensor_tensor(
-                    rotated[a, t][:], state[:, t, a, :], lr_t[:, col], by_li[:, 1 - a, :], ALU.mult, (ALU.subtract, ALU.add)[a]
-                )
+            rotate(t, parts, [by_li[:, a, :] for a in range(2)], [rotated[a, t][:] for a in range(2)])
 
         def gather_h(a, t, half):
             src = rotated[a, t][:].indirect(par_t[:, half * HALF // 16 : (half + 1) * HALF // 16])
@@ -150,90 +141,104 @@ def tile_picked_lru8_none_po_kernel(
             n = slice(first * P, last * P)
             nc.vector.quantize_mx(out=w_q[a][:, n].bitcast(FP8X4), scales=w_s[a][:, n], in_=w_bf[:])
 
-        for t in range(PACK):
-            rotate(t)
-        early = laid.tile([P, 3, PACK, HALF], F32, name="picked_early", offset=0, align_bytes=64)
-        picked = [[early[:, 0], early[:, 2]], [early[:, 1], None]]
-        for t in range(PACK):
-            for a in (IM, RE):
-                gather_h(a, t, 0)
-        for t in range(PACK):
-            gather_h(RE, t, 1)
-        nc.vector.tensor_copy(
-            v_s[:].rearrange("p (t c i) -> p c t i", t=PACK, i=8),
-            vs_raw[:].rearrange("p (c i t) -> p c t i", t=PACK, i=8),
-        )
+        raw0 = held.tile([P, 2, S], F32, name="raw0")
         for a in range(2):
-            halves = [round_w(a, first, first + 2, nc.vector.tensor_copy) for first in (0, 2)]
-            for n in range(2):
-                quant_w(a, 2 * n, 2 * n + 2, halves[n])
+            nc.scalar.activation(raw0[:, a, :], h01[a][:].indirect(par_t[:]), COPY)
+        rotate_before(1, [h01[a][:, S:] for a in range(2)])
+        for quad in range(QUADS):
+            move_x_scales(quad)
+        rotate_before(2, [h2[:, a, :] for a in range(2)])
+        by_li0 = held.tile([P, 2, S], F32, name="by_li0")
+        nc.scalar.activation(by_li0[:].rearrange("p a s -> p (a s)"), raw0[:].rearrange("p a s -> p (a s)"), COPY, scale=li_t[:, 0:1])
+        rotate_before(3, [h3[:, a, :] for a in range(2)])
+        nc.vector.scalar_tensor_tensor(
+            gathered[:, :2, 0, :], raw0[:, RE, :].rearrange("p (h s) -> p h s", h=2), lr_t[:, 0:1],
+            by_li0[:, IM, :].rearrange("p (h s) -> p h s", h=2), ALU.mult, ALU.subtract,
+        )
+
+        def rotate_im0(half):
+            cols = slice(half * HALF, (half + 1) * HALF)
+            nc.vector.scalar_tensor_tensor(picked[IM][half][:, 0, :], raw0[:, IM, cols], lr_t[:, 0:1], by_li0[:, RE, cols], ALU.mult, ALU.add)
+
+        rotate_im0(0)
+        for half, a in ((0, RE), (1, RE), (0, IM)):
+            for t in range(1, PACK):
+                gather_h(a, t, half)
+        nc.gpsimd.tensor_copy(
+            v_s[:].rearrange("p (t m) -> p t m", t=PACK),
+            vs_raw[:].rearrange("p (m t) -> p t m", t=PACK),
+        )
+        halves = [round_w(RE, first, first + 2, nc.vector.tensor_copy) for first in (0, 2)]
+        for n in range(2):
+            quant_w(RE, 2 * n, 2 * n + 2, halves[n])
         for half in range(2):
             nc.vector.tensor_copy(
                 xw_g[:, half * HALF : (half + 1) * HALF], xw[:].indirect(offs_t[:, half * HALF // 16 : (half + 1) * HALF // 16])
             )
         v_q = [held.tile([P, N], U32, name="v_q%d" % a, align_bytes=64) for a in range(2)]
-        for a in range(2):
-            nc.scalar.copy(
-                v_q[a][:].rearrange("p (t c i) -> p c t i", t=PACK, i=2),
-                v_raw[a][:].rearrange("p (c i t) -> p c t i", t=PACK, i=2),
-            )
-        picked[IM][1] = laid.tile([P, PACK, HALF], F32, name="picked_late", offset=16384, align_bytes=64)[:]
-        for t in range(PACK):
-            gather_h(IM, t, 1)
 
-        z_bf = [held.tile([P, 2, CHUNK * PACK], BF16, name="z_bf%d" % c, align_bytes=64) for c in range(CHUNKS)]
-        z_q = [held.tile([P, 2 * CHUNK], U32, name="z_q%d" % c, align_bytes=64) for c in range(CHUNKS)]
-        z_s = [held.tile([P, 2 * CHUNK], U8, name="z_s%d" % c, align_bytes=64) for c in range(CHUNKS)]
+        def deal_words(a):
+            nc.gpsimd.tensor_copy(v_q[a][:].rearrange("p (t m) -> p t m", t=PACK), v_raw[a][:].rearrange("p (m t) -> p t m", t=PACK))
+
+        z_bf = [held.tile([P, CHUNKS, CHUNK * PACK], BF16, name="z_bf%d" % a, align_bytes=64) for a in range(2)]
+        z_of = {(c, a): z_bf[a][:, c, :] for c in range(CHUNKS) for a in range(2)}
+        z_q = [held.tile([P, S], U32, name="z_q%d" % a, align_bytes=64) for a in range(2)]
+        z_s = [held.tile([P, S], U8, name="z_s%d" % a, align_bytes=64) for a in range(2)]
         y_bf = [held.tile([P, 2, CHUNK * PACK], BF16, name="y_bf%d" % n, align_bytes=64) for n in range(2)]
         y_q = [held.tile([P, 2 * CHUNK], U32, name="y_q%d" % n, align_bytes=64) for n in range(2)]
         out_rows = out_0.rearrange("(p t) s -> p t s", t=PACK)
 
-        def add_input(c, a):
+        in_bank = {}
+
+        def project_in(c, a):
             cols = slice(c * CHUNK, (c + 1) * CHUNK)
-            bank = psum.tile([P, PACK, CHUNK], F32, name="in%d_%d" % (c, a), tag="bank%d" % (2 * c + a))
+            bank = psum.tile([P, PACK, CHUNK], F32, name="in%d_%d" % (c, a), tag="bank%d" % BANK_IN[a][c])
             for t in range(PACK):
                 m = slice(t * P, (t + 1) * P)
                 nc.tensor.matmul_mx(
                     out=bank[:, t, :], lhsT=w_q[a][:, m].bitcast(FP8X4), lhsT_scale=w_s[a][:, m],
                     rhs=xw_g[:, cols].bitcast(FP8X4), rhs_scale=xs_p[:, cols], start=True, stop=True,
                 )
+            in_bank[c, a] = bank
+
+        def states(c, a):
+            return picked[a][c // 2][:, :, c % 2 * CHUNK : (c % 2 + 1) * CHUNK]
+
+        def add_input(c, a):
             nc.vector.tensor_tensor(
-                z_bf[c][:, a, :].rearrange("p (c i t) -> p c t i", t=PACK, i=2),
-                bank[:].rearrange("p t (c i) -> p c t i", i=2),
-                picked[a][c // 2][:, :, c % 2 * CHUNK : (c % 2 + 1) * CHUNK].rearrange("p t (c i) -> p c t i", i=2),
+                z_of[c, a].rearrange("p (c i t) -> p c t i", t=PACK, i=2),
+                in_bank[c, a][:].rearrange("p t (c i) -> p c t i", i=2),
+                states(c, a).rearrange("p t (c i) -> p c t i", i=2),
                 ALU.add,
             )
 
-        def quant_z(c, first, last):
+        def quant_z(a, first, last):
             n = slice(first * CHUNK, last * CHUNK)
             nc.vector.quantize_mx(
-                out=z_q[c][:, n].bitcast(FP8X4), scales=z_s[c][:, n], in_=z_bf[c][:, first:last, :].rearrange("p a n -> p (a n)")
+                out=z_q[a][:, n].bitcast(FP8X4), scales=z_s[a][:, n],
+                in_=z_of[first, a] if last - first == 1 else z_bf[a][:, first:last, :].rearrange("p c n -> p (c n)"),
             )
 
-        out_bank = {}
+        out_banks = {}
 
         def project_out(c, a):
+            banks = BANK_OUT[c]
+            share = PACK // len(banks)
             if a == RE:
-                out_bank[c] = psum.tile([P, PACK, CHUNK], F32, name="out%d" % c, tag="bank%d" % BANK_OUT[c])
-            n = slice(a * CHUNK, (a + 1) * CHUNK)
+                out_banks[c] = [psum.tile([P, share, CHUNK], F32, name="out%d_%d" % (c, b), tag="bank%d" % b) for b in banks]
+            n = slice(c * CHUNK, (c + 1) * CHUNK)
             for t in range(PACK):
                 m = slice(t * P, (t + 1) * P)
                 nc.tensor.matmul_mx(
-                    out=out_bank[c][:, t, :], lhsT=v_q[a][:, m].bitcast(FP8X4), lhsT_scale=v_s[4 * a : P, m],
-                    rhs=z_q[c][:, n].bitcast(FP8X4), rhs_scale=z_s[c][:, n],
-                    start=(a == RE and t == 0), stop=(a == IM and t == PACK - 1),
+                    out=out_banks[c][t // share][:, t % share, :], lhsT=v_q[a][:, m].bitcast(FP8X4), lhsT_scale=v_s[4 * a : P, m],
+                    rhs=z_q[a][:, n].bitcast(FP8X4), rhs_scale=z_s[a][:, n],
+                    start=(a == RE and t % share == 0), stop=(a == IM and t % share == share - 1),
                 )
 
-        def store_y(c):
-            y = held.tile([P, PACK, CHUNK], F32, name="y%d" % c)
-            nc.scalar.copy(y[:], out_bank[c][:])
-            nc.sync.dma_start(out_rows[:, :, c * CHUNK : (c + 1) * CHUNK], y[:])
+        y = [held.tile([P, PACK, CHUNK], F32, name="y%d" % c) for c in range(CHUNKS)]
 
-        def round_y(c, copy):
-            copy(
-                y_bf[c // 2][:, c % 2, :].rearrange("p (c i t) -> p c t i", t=PACK, i=2),
-                out_bank[c][:].rearrange("p t (c i) -> p c t i", i=2),
-            )
+        def store_y(c):
+            nc.sync.dma_start(out_rows[:, :, c * CHUNK : (c + 1) * CHUNK], y[c][:])
 
         def quant_y(first, last):
             n = slice(first % 2 * CHUNK, ((last - 1) % 2 + 1) * CHUNK)
@@ -246,52 +251,67 @@ def tile_picked_lru8_none_po_kernel(
             nc.sync.dma_start(as_words(out_1)[:, 2 * pair * CHUNK : 2 * (pair + 1) * CHUNK], y_q[pair][:].bitcast(I32))
 
         def finish(c):
-            project_out(c, RE)
             project_out(c, IM)
+            nc.scalar.copy(y[c][:], out_banks[c][0][:])
             store_y(c)
-            round_y(c, nc.scalar.copy)
 
+        def round_from_bank(c):
+            nc.scalar.copy(
+                y_bf[c // 2][:, c % 2, :].rearrange("p (c i t) -> p c t i", t=PACK, i=2),
+                out_banks[c][0][:].rearrange("p t (c i) -> p c t i", i=2),
+            )
+
+        deal_words(RE)
+        deal_words(IM)
+        for c in range(CHUNKS):
+            project_in(c, RE)
         add_input(0, RE)
-        add_input(0, IM)
         add_input(1, RE)
-        quant_z(0, 0, 2)
-        finish(0)
-        add_input(1, IM)
+        quant_z(RE, 0, 2)
+        project_out(0, RE)
+        project_out(1, RE)
+        quant_w(IM, 0, PACK, round_w(IM, 0, PACK, nc.scalar.copy))
+        z_late = laid.tile([P, 2, CHUNK * PACK], BF16, name="z_late", offset=4096, align_bytes=64)
+        z_of[2, RE], z_of[3, RE] = z_late[:, 0, :], z_late[:, 1, :]
+        picked[IM][1] = laid.tile([P, PACK, HALF], F32, name="picked_late", offset=0, align_bytes=64)[:]
+        for t in range(1, PACK):
+            gather_h(IM, t, 1)
         add_input(2, RE)
-        quant_z(1, 0, 2)
+        project_in(0, IM)
+        project_in(1, IM)
+        add_input(0, IM)
+        project_in(2, IM)
+        add_input(1, IM)
+        quant_z(IM, 0, 1)
+        finish(0)
+        round_from_bank(0)
+        rotate_im0(1)
+        quant_z(IM, 1, 2)
         finish(1)
+        round_from_bank(1)
+        project_in(3, IM)
         add_input(2, IM)
+        quant_z(RE, 2, 3)
+        project_out(2, RE)
         add_input(3, RE)
-        quant_z(2, 0, 2)
+        quant_z(IM, 2, 3)
         finish(2)
-        quant_z(3, 0, 1)
-        last = [psum.tile([P, 2, CHUNK], F32, name="last%d" % n, tag="bank%d" % (1, 3)[n]) for n in range(2)]
-
-        def project_last(a):
-            n = slice(a * CHUNK, (a + 1) * CHUNK)
-            for t in range(PACK):
-                m = slice(t * P, (t + 1) * P)
-                nc.tensor.matmul_mx(
-                    out=last[t // 2][:, t % 2, :], lhsT=v_q[a][:, m].bitcast(FP8X4), lhsT_scale=v_s[4 * a : P, m],
-                    rhs=z_q[3][:, n].bitcast(FP8X4), rhs_scale=z_s[3][:, n],
-                    start=(a == RE and t % 2 == 0), stop=(a == IM and t % 2 == 1),
-                )
-
-        project_last(RE)
         add_input(3, IM)
+        quant_z(RE, 3, 4)
+        project_out(3, RE)
+        quant_z(IM, 3, 4)
         quant_y(0, 2)
         store_words(0)
-        quant_z(3, 1, 2)
-        project_last(IM)
+        project_out(3, IM)
+        nc.scalar.copy(y[3][:, :2, :], out_banks[3][0][:])
+        nc.vector.tensor_copy(y[3][:, 2:, :], out_banks[3][1][:])
+        store_y(3)
+        for c in (2, 3):
+            nc.vector.tensor_copy(
+                y_bf[1][:, c % 2, :].rearrange("p (c i t) -> p c t i", t=PACK, i=4),
+                y[c][:].rearrange("p t (c i) -> p c t i", i=4),
+            )
         quant_y(2, 3)
-        y3 = held.tile([P, PACK, CHUNK], F32, name="y3")
-        nc.scalar.copy(y3[:, :2, :], last[0][:])
-        nc.vector.tensor_copy(y3[:, 2:, :], last[1][:])
-        nc.sync.dma_start(out_rows[:, :, 3 * CHUNK :], y3[:])
-        nc.vector.tensor_copy(
-            y_bf[1][:, 1, :].rearrange("p (c i t) -> p c t i", t=PACK, i=4),
-            y3[:].rearrange("p t (c i) -> p c t i", i=4),
-        )
         quant_y(3, 4)
         store_words(1)
         for quad in range(QUADS):

@@ -22,8 +22,8 @@ CHUNK = 128
 CHUNKS = S // CHUNK
 HALF = S // 2
 RE, IM = 0, 1
-BANK_IN = ((0, 1, 2, 3), (4, 5, 6, 7))
-BANK_OUT = ((0,), (1,), (2,), (3, 4))
+BANK_IN = ((0, 1, 2, 2), (4, 5, 6, 7))
+BANK_OUT = ((0,), (1,), (3,), (2, 4))
 
 
 def tile_picked_lru8_none_po_kernel(
@@ -50,14 +50,13 @@ def tile_picked_lru8_none_po_kernel(
         h01 = [held.tile([P, 2 * S], F32, name="h01_%d" % a) for a in range(2)]
         h2 = held.tile([P, 2, S], F32, name="h2")
         h3 = held.tile([P, 2, S], F32, name="h3")
-        w_raw = [held.tile([P, PACK, H], F32, name="w_raw0"), laid.tile([P, PACK, H], F32, name="w_raw1", offset=0, align_bytes=64)]
-        gathered = held.tile([P, 3, PACK, HALF], F32, name="gathered", align_bytes=64)
-        picked = [[gathered[:, 0], gathered[:, 1]], [gathered[:, 2], None]]
+        w_raw = [laid.tile([P, PACK, H], F32, name="w_raw%d" % a, offset=8192 * (1 - a), align_bytes=64) for a in range(2)]
+        picked_re = held.tile([P, PACK, S], F32, name="picked_re", align_bytes=64)
+        picked_im = [held.tile([P, PACK, HALF], F32, name="picked_im", align_bytes=64), None]
         w_q = [held.tile([P, H], U32, name="w_q%d" % a, align_bytes=64) for a in range(2)]
         w_s = [held.tile([P, H], U8, name="w_s%d" % a, align_bytes=64) for a in range(2)]
         v_raw = [held.tile([P, N], U32, name="v_raw%d" % a, align_bytes=64) for a in range(2)]
         vs_raw = held.tile([P, N], U8, name="vs_raw", align_bytes=64)
-        v_s = held.tile([P, N], U8, name="v_s", align_bytes=64)
         y_s = held.tile([P, S], U8, name="y_s", align_bytes=64)
 
         h_rows = [h.rearrange("(p t) s -> p t s", t=PACK) for h in (hr, hi)]
@@ -76,7 +75,7 @@ def tile_picked_lru8_none_po_kernel(
 
         def move_x_scales(quad):
             first = 32 * quad
-            nc.gpsimd.dma_start(xs_p[first : first + 4, :].bitcast(I32), xs_g[first : first + 32 : 8, :].bitcast(I32))
+            nc.sync.dma_start(xs_p[first : first + 4, :].bitcast(I32), xs_g[first : first + 32 : 8, :].bitcast(I32))
 
         def load_v_scales(a, quad):
             first = 32 * quad + 4 * a
@@ -99,78 +98,59 @@ def tile_picked_lru8_none_po_kernel(
         load_v_scales(RE, 0)
         load_v_scales(RE, 1)
         nc.sync.dma_start(xw[:].bitcast(I32), as_words(x_words))
+        nc.vector.tensor_copy(xs_g[:], xs[:].indirect(offs_t[:]))
+        for quad in range(QUADS):
+            move_x_scales(quad)
         load_v_scales(RE, 2)
         load_v_scales(RE, 3)
+        load_w(IM)
         for quad in range(QUADS):
             load_v_scales(IM, quad)
-        load_w(IM)
         for a in range(2):
             nc.sync.dma_start(v_raw[a][:].bitcast(I32), as_words((w3_words, w4_words)[a]))
-        nc.vector.tensor_copy(xs_g[:], xs[:].indirect(offs_t[:]))
 
-        def rotate(t, parts, by_li, dst):
-            for a in (IM, RE):
-                nc.vector.scalar_tensor_tensor(dst[a], parts[a], lr_t[:, t : t + 1], by_li[1 - a], ALU.mult, (ALU.subtract, ALU.add)[a])
-
-        rotated = {}
+        window = {}
 
         def rotate_before(t, parts):
-            by_li = held.tile([P, 2, S], F32, name="by_li%d" % t)
-            for a in range(2):
-                if t == 1:
-                    nc.gpsimd.tensor_scalar(by_li[:, a, :], parts[a], li_t[:, t : t + 1], 0.0, ALU.mult, ALU.add)
-                else:
-                    nc.vector.tensor_scalar(by_li[:, a, :], parts[a], li_t[:, t : t + 1], None, ALU.mult)
-            for a in range(2):
-                rotated[a, t] = held.tile([P, S], F32, name="rot%d_%d" % (a, t))
-            rotate(t, parts, [by_li[:, a, :] for a in range(2)], [rotated[a, t][:] for a in range(2)])
+            col = slice(t, t + 1)
+            window[RE, t] = held.tile([P, 2 * S], F32, name="window_re%d" % t)
+            window[IM, t] = held.tile([P, S], F32, name="window_im%d" % t)
+            li_hr = held.tile([P, S], F32, name="li_hr%d" % t)
+            for dst, a in ((li_hr[:], RE), (window[RE, t][:, S:], IM)):
+                nc.vector.tensor_scalar(dst, parts[a], li_t[:, col], None, ALU.mult)
+            nc.vector.scalar_tensor_tensor(window[IM, t][:], parts[IM], lr_t[:, col], li_hr[:], ALU.mult, ALU.add)
+            nc.vector.scalar_tensor_tensor(window[RE, t][:, :S], parts[RE], lr_t[:, col], window[RE, t][:, S:], ALU.mult, ALU.subtract)
 
-        def gather_h(a, t, half):
-            src = rotated[a, t][:].indirect(par_t[:, half * HALF // 16 : (half + 1) * HALF // 16])
-            nc.scalar.activation(picked[a][half][:, t, :], src, COPY)
+        def gather_im(t, half):
+            src = window[IM, t][:].indirect(par_t[:, half * HALF // 16 : (half + 1) * HALF // 16])
+            nc.scalar.activation(picked_im[half][:, t, :], src, COPY)
 
-        def round_w(a, first, last, copy):
-            w_bf = held.tile([P, (last - first) * P * PACK], BF16, name="w_bf%d_%d" % (a, first), align_bytes=64)
-            copy(
-                w_bf[:].rearrange("p (t m h l) -> p m h t l", m=P, h=2, l=2),
-                w_raw[a][:].rearrange("p (h l) (m t) -> p m h t l", t=PACK, l=2)[:, :, :, first:last, :],
-            )
-            return w_bf
-
-        def quant_w(a, first, last, w_bf):
-            n = slice(first * P, last * P)
-            nc.vector.quantize_mx(out=w_q[a][:, n].bitcast(FP8X4), scales=w_s[a][:, n], in_=w_bf[:])
+        def quant_w(a, w_bf):
+            nc.vector.quantize_mx(out=w_q[a][:].bitcast(FP8X4), scales=w_s[a][:], in_=w_bf[:])
 
         raw0 = held.tile([P, 2, S], F32, name="raw0")
         for a in range(2):
             nc.scalar.activation(raw0[:, a, :], h01[a][:].indirect(par_t[:]), COPY)
         rotate_before(1, [h01[a][:, S:] for a in range(2)])
-        for quad in range(QUADS):
-            move_x_scales(quad)
         rotate_before(2, [h2[:, a, :] for a in range(2)])
         by_li0 = held.tile([P, 2, S], F32, name="by_li0")
         nc.scalar.activation(by_li0[:].rearrange("p a s -> p (a s)"), raw0[:].rearrange("p a s -> p (a s)"), COPY, scale=li_t[:, 0:1])
         rotate_before(3, [h3[:, a, :] for a in range(2)])
-        nc.vector.scalar_tensor_tensor(
-            gathered[:, :2, 0, :], raw0[:, RE, :].rearrange("p (h s) -> p h s", h=2), lr_t[:, 0:1],
-            by_li0[:, IM, :].rearrange("p (h s) -> p h s", h=2), ALU.mult, ALU.subtract,
-        )
+        nc.vector.scalar_tensor_tensor(picked_re[:, 0, :], raw0[:, RE, :], lr_t[:, 0:1], by_li0[:, IM, :], ALU.mult, ALU.subtract)
 
         def rotate_im0(half):
             cols = slice(half * HALF, (half + 1) * HALF)
-            nc.vector.scalar_tensor_tensor(picked[IM][half][:, 0, :], raw0[:, IM, cols], lr_t[:, 0:1], by_li0[:, RE, cols], ALU.mult, ALU.add)
+            nc.vector.scalar_tensor_tensor(picked_im[half][:, 0, :], raw0[:, IM, cols], lr_t[:, 0:1], by_li0[:, RE, cols], ALU.mult, ALU.add)
 
         rotate_im0(0)
-        for half, a in ((0, RE), (1, RE), (0, IM)):
-            for t in range(1, PACK):
-                gather_h(a, t, half)
-        nc.gpsimd.tensor_copy(
-            v_s[:].rearrange("p (t m) -> p t m", t=PACK),
-            vs_raw[:].rearrange("p (m t) -> p t m", t=PACK),
+        for t in range(1, PACK):
+            nc.scalar.activation(picked_re[:, t, :], window[RE, t][:].indirect(par_t[:]), COPY)
+            gather_im(t, 0)
+        w_bf = [held.tile([P, H * PACK], BF16, name="w_bf%d" % a, align_bytes=64) for a in range(2)]
+        nc.vector.tensor_copy(
+            w_bf[RE][:].rearrange("p (t m j) -> p m t j", t=PACK, j=PACK), w_raw[RE][:].rearrange("p j (m t) -> p m t j", t=PACK)
         )
-        halves = [round_w(RE, first, first + 2, nc.vector.tensor_copy) for first in (0, 2)]
-        for n in range(2):
-            quant_w(RE, 2 * n, 2 * n + 2, halves[n])
+        quant_w(RE, w_bf[RE])
         for half in range(2):
             nc.vector.tensor_copy(
                 xw_g[:, half * HALF : (half + 1) * HALF], xw[:].indirect(offs_t[:, half * HALF // 16 : (half + 1) * HALF // 16])
@@ -178,7 +158,10 @@ def tile_picked_lru8_none_po_kernel(
         v_q = [held.tile([P, N], U32, name="v_q%d" % a, align_bytes=64) for a in range(2)]
 
         def deal_words(a):
-            nc.gpsimd.tensor_copy(v_q[a][:].rearrange("p (t m) -> p t m", t=PACK), v_raw[a][:].rearrange("p (m t) -> p t m", t=PACK))
+            nc.scalar.copy(
+                v_q[a][:].rearrange("p (t c i) -> p c t i", t=PACK, i=2),
+                v_raw[a][:].rearrange("p (c i t) -> p c t i", t=PACK, i=2),
+            )
 
         z_bf = [held.tile([P, CHUNKS, CHUNK * PACK], BF16, name="z_bf%d" % a, align_bytes=64) for a in range(2)]
         z_of = {(c, a): z_bf[a][:, c, :] for c in range(CHUNKS) for a in range(2)}
@@ -202,7 +185,9 @@ def tile_picked_lru8_none_po_kernel(
             in_bank[c, a] = bank
 
         def states(c, a):
-            return picked[a][c // 2][:, :, c % 2 * CHUNK : (c % 2 + 1) * CHUNK]
+            if a == RE:
+                return picked_re[:, :, c * CHUNK : (c + 1) * CHUNK]
+            return picked_im[c // 2][:, :, c % 2 * CHUNK : (c % 2 + 1) * CHUNK]
 
         def add_input(c, a):
             nc.vector.tensor_tensor(
@@ -255,32 +240,47 @@ def tile_picked_lru8_none_po_kernel(
             nc.scalar.copy(y[c][:], out_banks[c][0][:])
             store_y(c)
 
+        def round_rows(c):
+            nc.vector.tensor_copy(
+                y_bf[c // 2][:, c % 2, :].rearrange("p (c i t) -> p c t i", t=PACK, i=4),
+                y[c][:].rearrange("p t (c i) -> p c t i", i=4),
+            )
+
         def round_from_bank(c):
             nc.scalar.copy(
                 y_bf[c // 2][:, c % 2, :].rearrange("p (c i t) -> p c t i", t=PACK, i=2),
                 out_banks[c][0][:].rearrange("p t (c i) -> p c t i", i=2),
             )
 
+        for c in range(CHUNKS - 1):
+            project_in(c, RE)
+            add_input(c, RE)
+        project_in(3, RE)
+        quant_z(RE, 0, 2)
+        quant_z(RE, 2, 3)
+        nc.scalar.copy(
+            w_bf[IM][:].rearrange("p (t m h l) -> p m h t l", t=PACK, h=2, l=2),
+            w_raw[IM][:].rearrange("p (h l) (m t) -> p m h t l", t=PACK, l=2),
+        )
+        quant_w(IM, w_bf[IM])
+        v_s = laid.tile([P, N], U8, name="v_s", offset=6144, align_bytes=64)
+        nc.vector.tensor_copy(
+            v_s[:].rearrange("p (t c i) -> p c t i", t=PACK, i=8),
+            vs_raw[:].rearrange("p (c i t) -> p c t i", t=PACK, i=8),
+        )
         deal_words(RE)
         deal_words(IM)
-        for c in range(CHUNKS):
-            project_in(c, RE)
-        add_input(0, RE)
-        add_input(1, RE)
-        quant_z(RE, 0, 2)
-        project_out(0, RE)
-        project_out(1, RE)
-        quant_w(IM, 0, PACK, round_w(IM, 0, PACK, nc.scalar.copy))
-        z_late = laid.tile([P, 2, CHUNK * PACK], BF16, name="z_late", offset=4096, align_bytes=64)
-        z_of[2, RE], z_of[3, RE] = z_late[:, 0, :], z_late[:, 1, :]
-        picked[IM][1] = laid.tile([P, PACK, HALF], F32, name="picked_late", offset=0, align_bytes=64)[:]
+        z_of[3, RE] = laid.tile([P, CHUNK * PACK], BF16, name="z_late", offset=4096, align_bytes=64)[:]
+        picked_im[1] = laid.tile([P, PACK, HALF], F32, name="picked_late", offset=0, align_bytes=64)
         for t in range(1, PACK):
-            gather_h(IM, t, 1)
-        add_input(2, RE)
+            gather_im(t, 1)
+        add_input(3, RE)
         project_in(0, IM)
         project_in(1, IM)
+        project_out(0, RE)
         add_input(0, IM)
         project_in(2, IM)
+        project_out(1, RE)
         add_input(1, IM)
         quant_z(IM, 0, 1)
         finish(0)
@@ -288,17 +288,15 @@ def tile_picked_lru8_none_po_kernel(
         rotate_im0(1)
         quant_z(IM, 1, 2)
         finish(1)
-        round_from_bank(1)
         project_in(3, IM)
-        add_input(2, IM)
-        quant_z(RE, 2, 3)
         project_out(2, RE)
-        add_input(3, RE)
+        add_input(2, IM)
+        quant_z(RE, 3, 4)
+        project_out(3, RE)
         quant_z(IM, 2, 3)
         finish(2)
         add_input(3, IM)
-        quant_z(RE, 3, 4)
-        project_out(3, RE)
+        round_rows(1)
         quant_z(IM, 3, 4)
         quant_y(0, 2)
         store_words(0)
@@ -306,11 +304,8 @@ def tile_picked_lru8_none_po_kernel(
         nc.scalar.copy(y[3][:, :2, :], out_banks[3][0][:])
         nc.vector.tensor_copy(y[3][:, 2:, :], out_banks[3][1][:])
         store_y(3)
-        for c in (2, 3):
-            nc.vector.tensor_copy(
-                y_bf[1][:, c % 2, :].rearrange("p (c i t) -> p c t i", t=PACK, i=4),
-                y[c][:].rearrange("p t (c i) -> p c t i", i=4),
-            )
+        round_rows(2)
+        round_rows(3)
         quant_y(2, 3)
         quant_y(3, 4)
         store_words(1)

from contextlib import ExitStack

import concourse.mybir as mybir

T, S, N, H = 2048, 512, 512, 512
FLOPS = 4 * 2 * 512 * 512 * 512

F32 = mybir.dt.float32
BF16 = mybir.dt.bfloat16
I32 = mybir.dt.int32
U32 = mybir.dt.uint32
U16 = mybir.dt.uint16
U8 = mybir.dt.uint8
FP8X4 = mybir.dt.float8_e4m3fn_x4
ALU = mybir.AluOpType
COPY = mybir.ActivationFunctionType.Copy

P = 128
PACK = 4
QUADS = 4
CHUNK = 128
CHUNKS = S // CHUNK
HALF = S // 2
RE, IM = 0, 1
BANK_IN = ((0, 1, 2, 2), (4, 5, 6, 7))
BANK_OUT = ((0,), (1,), (3,), (2, 4))


def tile_picked_lru8_none_po_kernel(
    tc, x_words, x_scales, w1, w2, hr, hi, lr, li, w3_words, w3_scales, w4_words, w4_scales, offs, par, out_0, out_1, out_2
):
    nc = tc.nc
    with ExitStack() as ctx:
        held = ctx.enter_context(tc.tile_pool(name="held", bufs=1))
        laid = ctx.enter_context(tc.tile_pool(name="laid", bufs=1))
        psum = ctx.enter_context(tc.psum_pool(name="psum", bufs=1))

        def as_words(packed):
            return packed[0].rearrange("p n t -> p (n t)").bitcast(I32)

        offs_t = held.tile([P, S // 16], U16, name="offs_t")
        par_t = held.tile([P, S // 16], U16, name="par_t")
        lr_t = held.tile([P, PACK], F32, name="lr_t")
        li_t = held.tile([P, PACK], F32, name="li_t")
        xw = held.tile([P, T], U32, name="xw")
        xs = held.tile([P, T], U8, name="xs", align_bytes=64)
        xw_g = held.tile([P, S], U32, name="xw_g", align_bytes=64)
        xs_g = held.tile([P, S], U8, name="xs_g", align_bytes=64)
        xs_p = held.tile([P, S], U8, name="xs_p", align_bytes=64)
        h01 = [held.tile([P, 2 * S], F32, name="h01_%d" % a) for a in range(2)]
        h2 = held.tile([P, 2, S], F32, name="h2")
        h3 = held.tile([P, 2, S], F32, name="h3")
        w_raw = [laid.tile([P, PACK, H], F32, name="w_raw%d" % a, offset=8192 * (1 - a), align_bytes=64) for a in range(2)]
        picked_re = held.tile([P, PACK, S], F32, name="picked_re", align_bytes=64)
        picked_im = [held.tile([P, PACK, HALF], F32, name="picked_im", align_bytes=64), None]
        w_q = [held.tile([P, H], U32, name="w_q%d" % a, align_bytes=64) for a in range(2)]
        w_s = [held.tile([P, H], U8, name="w_s%d" % a, align_bytes=64) for a in range(2)]
        v_raw = [held.tile([P, N], U32, name="v_raw%d" % a, align_bytes=64) for a in range(2)]
        vs_raw = held.tile([P, N], U8, name="vs_raw", align_bytes=64)
        y_s = held.tile([P, S], U8, name="y_s", align_bytes=64)

        h_rows = [h.rearrange("(p t) s -> p t s", t=PACK) for h in (hr, hi)]
        w_rows = [w.rearrange("(p j) c -> p j c", j=PACK) for w in (w1, w2)]

        warm_in = held.tile([P, 1], F32, name="warm")
        warm_out = held.tile([P, 1], F32, name="warm2")
        nc.vector.memset(warm_in[:], 0.0)
        nc.scalar.activation(warm_out[:], warm_in[:], COPY)
        nc.vector.memset(xs[:].bitcast(I32), 0)
        nc.vector.memset(xs_p[:].bitcast(I32), 0)
        nc.vector.memset(vs_raw[:].bitcast(I32), 0)

        def load_w(a):
            nc.sync.dma_start(w_raw[a][:], w_rows[a])

        def move_x_scales(quad):
            first = 32 * quad
            nc.sync.dma_start(xs_p[first : first + 4, :].bitcast(I32), xs_g[first : first + 32 : 8, :].bitcast(I32))

        def load_v_scales(a, quad):
            first = 32 * quad + 4 * a
            nc.sync.dma_start(
                vs_raw[first : first + 4, :].bitcast(I32), (w3_scales, w4_scales)[a][0, 4 * quad : 4 * quad + 4, :].bitcast(I32)
            )

        nc.sync.dma_start(par_t[:], par)
        nc.sync.dma_start(li_t[:], li.rearrange("(p t) o -> p (t o)", t=PACK))
        nc.sync.dma_start(h01[RE][:].rearrange("p (t s) -> p t s", t=2), h_rows[RE][:, :2, :])
        nc.sync.dma_start(offs_t[:], offs)
        nc.sync.dma_start(xs[0:P:8, :].bitcast(I32), x_scales[0].bitcast(I32))
        nc.sync.dma_start(h01[IM][:, S:], h_rows[IM][:, 1, :])
        nc.sync.dma_start(lr_t[:], lr.rearrange("(p t) o -> p (t o)", t=PACK))
        nc.sync.dma_start(h01[IM][:, :S], h_rows[IM][:, 0, :])
        for t, h_t in ((2, h2), (3, h3)):
            for a in range(2):
                nc.sync.dma_start(h_t[:, a, :], h_rows[a][:, t, :])
        load_w(RE)
        load_v_scales(RE, 0)
        load_v_scales(RE, 1)
        nc.sync.dma_start(xw[:].bitcast(I32), as_words(x_words))
        nc.vector.tensor_copy(xs_g[:], xs[:].indirect(offs_t[:]))
        for quad in range(QUADS):
            move_x_scales(quad)
        load_v_scales(RE, 2)
        load_v_scales(RE, 3)
        load_w(IM)
        for quad in range(QUADS):
            load_v_scales(IM, quad)
        for a in range(2):
            nc.sync.dma_start(v_raw[a][:].bitcast(I32), as_words((w3_words, w4_words)[a]))

        window = {}

        def rotate_before(t, parts):
            col = slice(t, t + 1)
            window[RE, t] = held.tile([P, 2 * S], F32, name="window_re%d" % t)
            window[IM, t] = held.tile([P, S], F32, name="window_im%d" % t)
            li_hr = held.tile([P, S], F32, name="li_hr%d" % t)
            for dst, a in ((li_hr[:], RE), (window[RE, t][:, S:], IM)):
                nc.vector.tensor_scalar(dst, parts[a], li_t[:, col], None, ALU.mult)
            nc.vector.scalar_tensor_tensor(window[IM, t][:], parts[IM], lr_t[:, col], li_hr[:], ALU.mult, ALU.add)
            nc.vector.scalar_tensor_tensor(window[RE, t][:, :S], parts[RE], lr_t[:, col], window[RE, t][:, S:], ALU.mult, ALU.subtract)

        def gather_im(t, half):
            src = window[IM, t][:].indirect(par_t[:, half * HALF // 16 : (half + 1) * HALF // 16])
            nc.scalar.activation(picked_im[half][:, t, :], src, COPY)

        def quant_w(a, w_bf):
            nc.vector.quantize_mx(out=w_q[a][:].bitcast(FP8X4), scales=w_s[a][:], in_=w_bf[:])

        raw0 = held.tile([P, 2, S], F32, name="raw0")
        for a in range(2):
            nc.scalar.activation(raw0[:, a, :], h01[a][:].indirect(par_t[:]), COPY)
        rotate_before(1, [h01[a][:, S:] for a in range(2)])
        rotate_before(2, [h2[:, a, :] for a in range(2)])
        by_li0 = held.tile([P, 2, S], F32, name="by_li0")
        nc.scalar.activation(by_li0[:].rearrange("p a s -> p (a s)"), raw0[:].rearrange("p a s -> p (a s)"), COPY, scale=li_t[:, 0:1])
        rotate_before(3, [h3[:, a, :] for a in range(2)])
        nc.vector.scalar_tensor_tensor(picked_re[:, 0, :], raw0[:, RE, :], lr_t[:, 0:1], by_li0[:, IM, :], ALU.mult, ALU.subtract)

        def rotate_im0(half):
            cols = slice(half * HALF, (half + 1) * HALF)
            nc.vector.scalar_tensor_tensor(picked_im[half][:, 0, :], raw0[:, IM, cols], lr_t[:, 0:1], by_li0[:, RE, cols], ALU.mult, ALU.add)

        rotate_im0(0)
        for t in range(1, PACK):
            nc.scalar.activation(picked_re[:, t, :], window[RE, t][:].indirect(par_t[:]), COPY)
            gather_im(t, 0)
        w_bf = [held.tile([P, H * PACK], BF16, name="w_bf%d" % a, align_bytes=64) for a in range(2)]
        nc.vector.tensor_copy(
            w_bf[RE][:].rearrange("p (t m j) -> p m t j", t=PACK, j=PACK), w_raw[RE][:].rearrange("p j (m t) -> p m t j", t=PACK)
        )
        quant_w(RE, w_bf[RE])
        for half in range(2):
            nc.vector.tensor_copy(
                xw_g[:, half * HALF : (half + 1) * HALF], xw[:].indirect(offs_t[:, half * HALF // 16 : (half + 1) * HALF // 16])
            )
        v_q = [held.tile([P, N], U32, name="v_q%d" % a, align_bytes=64) for a in range(2)]

        def deal_words(a):
            nc.scalar.copy(
                v_q[a][:].rearrange("p (t c i) -> p c t i", t=PACK, i=2),
                v_raw[a][:].rearrange("p (c i t) -> p c t i", t=PACK, i=2),
            )

        z_bf = [held.tile([P, CHUNKS, CHUNK * PACK], BF16, name="z_bf%d" % a, align_bytes=64) for a in range(2)]
        z_of = {(c, a): z_bf[a][:, c, :] for c in range(CHUNKS) for a in range(2)}
        z_q = [held.tile([P, S], U32, name="z_q%d" % a, align_bytes=64) for a in range(2)]
        z_s = [held.tile([P, S], U8, name="z_s%d" % a, align_bytes=64) for a in range(2)]
        y_bf = [held.tile([P, 2, CHUNK * PACK], BF16, name="y_bf%d" % n, align_bytes=64) for n in range(2)]
        y_q = [held.tile([P, 2 * CHUNK], U32, name="y_q%d" % n, align_bytes=64) for n in range(2)]
        out_rows = out_0.rearrange("(p t) s -> p t s", t=PACK)

        in_bank = {}

        def project_in(c, a):
            cols = slice(c * CHUNK, (c + 1) * CHUNK)
            bank = psum.tile([P, PACK, CHUNK], F32, name="in%d_%d" % (c, a), tag="bank%d" % BANK_IN[a][c])
            for t in range(PACK):
                m = slice(t * P, (t + 1) * P)
                nc.tensor.matmul_mx(
                    out=bank[:, t, :], lhsT=w_q[a][:, m].bitcast(FP8X4), lhsT_scale=w_s[a][:, m],
                    rhs=xw_g[:, cols].bitcast(FP8X4), rhs_scale=xs_p[:, cols], start=True, stop=True,
                )
            in_bank[c, a] = bank

        def states(c, a):
            if a == RE:
                return picked_re[:, :, c * CHUNK : (c + 1) * CHUNK]
            return picked_im[c // 2][:, :, c % 2 * CHUNK : (c % 2 + 1) * CHUNK]

        def add_input(c, a):
            nc.vector.tensor_tensor(
                z_of[c, a].rearrange("p (c i t) -> p c t i", t=PACK, i=2),
                in_bank[c, a][:].rearrange("p t (c i) -> p c t i", i=2),
                states(c, a).rearrange("p t (c i) -> p c t i", i=2),
                ALU.add,
            )

        def quant_z(a, first, last):
            n = slice(first * CHUNK, last * CHUNK)
            nc.vector.quantize_mx(
                out=z_q[a][:, n].bitcast(FP8X4), scales=z_s[a][:, n],
                in_=z_of[first, a] if last - first == 1 else z_bf[a][:, first:last, :].rearrange("p c n -> p (c n)"),
            )

        out_banks = {}

        def project_out(c, a):
            banks = BANK_OUT[c]
            share = PACK // len(banks)
            if a == RE:
                out_banks[c] = [psum.tile([P, share, CHUNK], F32, name="out%d_%d" % (c, b), tag="bank%d" % b) for b in banks]
            n = slice(c * CHUNK, (c + 1) * CHUNK)
            for t in range(PACK):
                m = slice(t * P, (t + 1) * P)
                nc.tensor.matmul_mx(
                    out=out_banks[c][t // share][:, t % share, :], lhsT=v_q[a][:, m].bitcast(FP8X4), lhsT_scale=v_s[4 * a : P, m],
                    rhs=z_q[a][:, n].bitcast(FP8X4), rhs_scale=z_s[a][:, n],
                    start=(a == RE and t % share == 0), stop=(a == IM and t % share == share - 1),
                )

        y = [held.tile([P, PACK, CHUNK], F32, name="y%d" % c) for c in range(CHUNKS)]

        def store_y(c):
            nc.sync.dma_start(out_rows[:, :, c * CHUNK : (c + 1) * CHUNK], y[c][:])

        def quant_y(first, last):
            n = slice(first % 2 * CHUNK, ((last - 1) % 2 + 1) * CHUNK)
            nc.vector.quantize_mx(
                out=y_q[first // 2][:, n].bitcast(FP8X4), scales=y_s[:, first * CHUNK : last * CHUNK],
                in_=y_bf[first // 2][:, first % 2 : (last - 1) % 2 + 1, :].rearrange("p h n -> p (h n)"),
            )

        def store_words(pair):
            nc.sync.dma_start(as_words(out_1)[:, 2 * pair * CHUNK : 2 * (pair + 1) * CHUNK], y_q[pair][:].bitcast(I32))

        def finish(c):
            project_out(c, IM)
            nc.scalar.copy(y[c][:], out_banks[c][0][:])
            store_y(c)

        def round_rows(c):
            nc.vector.tensor_copy(
                y_bf[c // 2][:, c % 2, :].rearrange("p (c i t) -> p c t i", t=PACK, i=4),
                y[c][:].rearrange("p t (c i) -> p c t i", i=4),
            )

        def round_from_bank(c):
            nc.scalar.copy(
                y_bf[c // 2][:, c % 2, :].rearrange("p (c i t) -> p c t i", t=PACK, i=2),
                out_banks[c][0][:].rearrange("p t (c i) -> p c t i", i=2),
            )

        for c in range(CHUNKS - 1):
            project_in(c, RE)
            add_input(c, RE)
        project_in(3, RE)
        quant_z(RE, 0, 2)
        quant_z(RE, 2, 3)
        nc.scalar.copy(
            w_bf[IM][:].rearrange("p (t m h l) -> p m h t l", t=PACK, h=2, l=2),
            w_raw[IM][:].rearrange("p (h l) (m t) -> p m h t l", t=PACK, l=2),
        )
        quant_w(IM, w_bf[IM])
        v_s = laid.tile([P, N], U8, name="v_s", offset=6144, align_bytes=64)
        nc.vector.tensor_copy(
            v_s[:].rearrange("p (t c i) -> p c t i", t=PACK, i=8),
            vs_raw[:].rearrange("p (c i t) -> p c t i", t=PACK, i=8),
        )
        deal_words(RE)
        deal_words(IM)
        z_of[3, RE] = laid.tile([P, CHUNK * PACK], BF16, name="z_late", offset=4096, align_bytes=64)[:]
        picked_im[1] = laid.tile([P, PACK, HALF], F32, name="picked_late", offset=0, align_bytes=64)
        for t in range(1, PACK):
            gather_im(t, 1)
        add_input(3, RE)
        project_in(0, IM)
        project_in(1, IM)
        project_out(0, RE)
        add_input(0, IM)
        project_in(2, IM)
        project_out(1, RE)
        add_input(1, IM)
        quant_z(IM, 0, 1)
        finish(0)
        round_from_bank(0)
        rotate_im0(1)
        quant_z(IM, 1, 2)
        finish(1)
        project_in(3, IM)
        project_out(2, RE)
        add_input(2, IM)
        quant_z(RE, 3, 4)
        project_out(3, RE)
        quant_z(IM, 2, 3)
        finish(2)
        add_input(3, IM)
        round_rows(1)
        quant_z(IM, 3, 4)
        quant_y(0, 2)
        store_words(0)
        project_out(3, IM)
        nc.scalar.copy(y[3][:, :2, :], out_banks[3][0][:])
        nc.vector.tensor_copy(y[3][:, 2:, :], out_banks[3][1][:])
        store_y(3)
        round_rows(2)
        round_rows(3)
        quant_y(2, 3)
        quant_y(3, 4)
        store_words(1)
        for quad in range(QUADS):
            (nc.sync, nc.scalar)[quad % 2].dma_start(
                out_2[0, 4 * quad : 4 * quad + 4, :].bitcast(I32), y_s[32 * quad : 32 * quad + 4, :].bitcast(I32)
            )
